import numpy as np, ml_dtypes
CORES = [2,3,42,43,82,83,122,123]
N = 8
BF = ml_dtypes.bfloat16
V, HV, LV, K, T, S, EPS, LK = 4096, 2048, 12, 192, 4, 3, 60, 8
def pick(tab, ix):
    return np.take_along_axis(tab, ix[:, :, None, :], 3)
def parts(rng):
    px = np.clip(rng.integers(0, 256, (1, 8, 16, V)) + rng.integers(-48, 49, (N, 8, 16, V)), 0, 255)
    vi = rng.integers(0, V, (N, 8, 16, V))
    few = rng.integers(0, V, (N, 8, 16))
    v = np.where(rng.random((N, 8, K)) < 0.25, np.take_along_axis(few, rng.integers(0, 16, (N, 8, K)), 2), rng.integers(0, V, (N, 8, K)))
    near = np.clip(pick(px, v) + rng.integers(-120, 121, (N, 8, 16, K)), 0, 255)
    z = np.where(rng.random((N, 8, 1, K)) < 0.4, near, rng.integers(0, 256, (N, 8, 16, K)))
    f = rng.integers(0, V, (N, 8, 16, K)); d = rng.integers(0, 4, (N, 8, K))
    return px, vi, z, f, v, d, rng.integers(0, 256, (N, 8, 16)), rng.integers(0, 4096, (N, 8, 16))
def pack(px, vi, z, f, v, d, w, k):
    return {"px": np.ascontiguousarray(px.reshape(N, 128, V)).astype(np.float32).astype(BF), "vw": (vi[..., :HV] + V * vi[..., HV:]).reshape(N, 128, HV).astype(np.int32),
            "z0": z.reshape(N, 128, K).astype(np.float32).astype(BF), "f0": f.reshape(N, 128, K).astype(np.int32), "v0": v.astype(np.int32), "d0": d.astype(np.int32),
            "wt": w.reshape(N, 128, 1).astype(np.int32), "kap": k.reshape(N, 128, 1).astype(np.int32)}
def setup_inputs(rng):
    return pack(*parts(rng))
def setup_inputs_corners(rng):
    px, vi, z, f, v, d, w, k = parts(rng); own = np.arange(V)[None, :]; lane = np.arange(16); i = np.arange(K); one = 0 * i
    for r in range(N):
        for g in range(8):
            m = r + g
            d[r, g] = (one, one + 1, one + 3, 3 * (i & 1))[m & 3]
            v[r, g] = (one + (0, V - 1, HV)[m % 3], rng.permutation(V)[:K], (V - 1) * (i & 1), V - K + i)[(r + (g >> 1)) & 3]
            vi[r, g] = (own + 0 * lane[:, None], V - 1 - own + 0 * lane[:, None], (own + 1 + lane[:, None]) & (V - 1), (V - 1) * rng.integers(0, 2, (16, V)))[g & 3]
            f[r, g] = vi[r, g][:, v[r, g]] if m & 1 else (V - 1) * rng.integers(0, 2, (16, K))
            w[r, g] = (0 * lane, 0 * lane + 255, 255 * (lane == 15), w[r, g])[(m >> 1) & 3]
            k[r, g] = (0 * lane, 0 * lane + 4095, 4095 * (lane == 15), k[r, g])[(r + 3 * g) & 3]
            likes = (i >= 0, i < 0, (i & 1) == 0, (i & 1) == 1, rng.random(K) < 0.5)[(r + 2 * g) % 5]
            x = px[r, g][:, v[r, g]]; z[r, g] = np.where(likes[None, :], x, (x + 128) & 255)
    return pack(px, vi, z, f, v, d, w, k)
def setup_inputs_ends(rng):
    def bits(*shape):
        return rng.integers(0, 2, shape)
    pat = 255 * bits(N, 8, 16, 6); pat[..., 0] = 0; pat[..., 1] = 255; pat[..., 3] = 255 - pat[..., 2]
    px = np.take_along_axis(pat, rng.integers(0, 6, (N, 8, 1, V)), 3)
    px[..., 0] = 0; px[..., V - 1] = 255; px[..., V - 613] = 255
    vi = (V - 1) * bits(N, 8, 16, HV); vi = np.concatenate([vi, vi], axis=3)
    z = 255 * bits(N, 8, 16, K); f = (V - 1) * bits(N, 8, 16, K); v = (V - 1) * bits(N, 8, K); d = 3 * bits(N, 8, K)
    w = 255 * bits(N, 8, 16); w[:, 1::2] = 255; k = 4095 * bits(N, 8, 16); k[..., 15] = 4095
    for h in (0, K - 4):
        z[..., h] = 255; v[..., h] = V - 1
        z[..., h + 1] = 255; v[..., h + 1] = 0; d[..., h + 1] = 3
        z[..., h + 2] = 0; z[:, :, 0, h + 2] = 255; z[:, :, 1, h + 2] = 2; v[..., h + 2] = V - 1
        z[..., h + 3] = 0; v[..., h + 3] = V - 1
    return pack(px, vi, z, f, v, d, w, k)
def setup_inputs_spread(rng):
    px = np.minimum((np.exp2(8 * rng.random((N, 8, 1, V))) * rng.random((N, 8, 16, V))).astype(np.int64), 255)
    z = np.minimum((np.exp2(8 * rng.random((N, 8, 1, K))) * rng.random((N, 8, 16, K))).astype(np.int64), 255)
    vi = np.minimum((V * rng.random((N, 8, 16, V)) ** 3).astype(np.int64), V - 1)
    f = np.minimum((V * rng.random((N, 8, 16, K)) ** 4).astype(np.int64), V - 1)
    v = np.minimum((V * rng.random((N, 8, K)) ** 2).astype(np.int64), V - 1)
    d = np.minimum((4 * rng.random((N, 8, K)) ** 2).astype(np.int64), 3)
    w = np.minimum(np.exp2(8 * rng.random((N, 8, 16))).astype(np.int64), 255); k = np.minimum(np.exp2(12 * rng.random((N, 8, 16))).astype(np.int64), 4095)
    return pack(px, vi, z, f, v, d, w, k)
def setup_inputs_ties(rng):
    px, vi, z, f, v, d, w, k = parts(rng)
    pat = np.broadcast_to(rng.integers(0, 256, (1, 8, 16, 8)), (N, 8, 16, 8))
    px = np.take_along_axis(pat, rng.integers(0, 8, (N, 8, 1, V)), 3)
    v = np.take_along_axis(rng.integers(0, V, (N, 8, 24)), rng.integers(0, 24, (N, 8, K)), 2)
    x = pick(px, v); n = LK - rng.integers(0, 2, (N, 8, 1, K)); o = np.argsort(rng.random((N, 8, 16, K)), axis=2)
    far = EPS + (o >= n).astype(np.int64); z = np.where(x + far <= 255, x + far, x - far)
    vi = np.where(rng.random((N, 8, 16, V)) < 0.2, np.arange(V), vi)
    return pack(px, vi, z, f, v, d, w, k)
def check_inputs(d):
    bad = []
    for a, lo, hi in (("px", 0, 255), ("vw", 0, V * V - 1), ("z0", 0, 255), ("f0", 0, V - 1), ("v0", 0, V - 1), ("d0", 0, 3), ("wt", 0, 255), ("kap", 0, 4095)):
        x = np.asarray(d[a]).astype(np.float64)
        if not (np.min(x) >= lo and np.max(x) <= hi): bad.append("range of " + a)
        if not np.all(x == np.rint(x)): bad.append("whole numbers of " + a)
    return bad
def distances(X, ix, q):
    flat = ix.reshape(N, 8, 16 * K); out = np.zeros((N, 8, 16, K), np.int64)
    for i in range(16):
        out += np.abs(np.take_along_axis(X[:, :, i], flat, 2).reshape(N, 8, 16, K) - q[:, :, i][:, :, None, :])
    return out
def place(view, k):
    return np.take_along_axis(view, k[:, :, None, :], 2)[:, :, 0]
def reference(px, vw, z0, f0, v0, d0, wt, kap):
    X = px.astype(np.int64).reshape(N, 8, 16, V); packed = vw.astype(np.int64).reshape(N, 8, 16, HV)
    vi = np.concatenate([packed & (V - 1), packed >> LV], axis=3)
    z = z0.astype(np.int64).reshape(N, 8, 16, K); f = f0.astype(np.int64).reshape(N, 8, 16, K); v = v0.astype(np.int64); dl = d0.astype(np.int64); A = np.zeros((N, 8, K), np.int64)
    wl = wt.astype(np.int64).reshape(N, 8, 16, 1); kl = kap.astype(np.int64).reshape(N, 8, 16, 1); other = np.arange(K) ^ 1
    for t in range(T):
        x = pick(X, v); e = pick(vi, v)
        like = np.add.reduce((np.abs(x - z) <= EPS).astype(np.int64), axis=2) >= LK + (A & 1); L = like[:, :, None, :]
        u = np.add.reduce(wl * z, axis=2) & (V - 1)
        h = np.where(L, f, (((u[:, :, None, :] * kl) >> 5) + 613 * v[:, :, None, :]) & (V - 1))
        de = distances(X, e, x); dh = distances(X, h, np.where(L, x, z))
        e = np.where(L & (dh < de), h, e)
        for r in range(N):
            for g in range(8):
                j = np.flatnonzero(like[r, g]); users, first = np.unique(v[r, g, j], return_index=True)
                vi[r, g][:, users] = e[r, g][:, j[first]]
        z = np.where(L, (z + x) >> 1, z); A = A + like.astype(np.int64); dl = np.where(like, 0, dl + 1)
        s = np.add.reduce(z, axis=2)
        v = np.where(like, place(e, (s + t) & 15), place(h, np.argmin(dh, axis=2)))
        f = e; second = place(e, (s + t + 8) & 15)
        over = like[:, :, other] & (dl >= 2); O = over[:, :, None, :]
        z = np.where(O, z[..., other], z); f = np.where(O, f[..., other], f); A = np.where(over, A[..., other], A)
        v = np.where(over, second[..., other], v); dl = np.where(over, 0, dl)
        if t < T - 1: z, f, v, A, dl = [np.roll(a, S, axis=0) for a in (z, f, v, A, dl)]
    return {"yw": (vi[..., :HV] + V * vi[..., HV:]).reshape(N, 128, HV).astype(np.float32), "yz": z.reshape(N, 128, K).astype(np.float32), "yf": f.reshape(N, 128, K).astype(np.float32),
            "yv": v.astype(np.float32), "yc": (16 * A + dl).astype(np.float32)}

@@ -1,0 +1,697 @@
+from concourse.mybir import AluOpType as OP, ActivationFunctionType as AF
+
+NB, n = 2, 96
+M6, BIGM = 6, 12582912.0
+DT = {"F": "float32", "H": "bfloat16", "J": "int32", "U": "uint16"}
+EPE = True
+ABS_E, ABS_H = "SSS", "SSS"
+
+
+def ap(buf, c0, c1, st=1, r0=0, r1=128):
+    return ("ap", buf, r0, r1, c0, c1, st)
+
+
+def sub(a, c0, c1, st=1):
+    return ("ap", a[1], a[2], a[3], a[4] + c0, a[4] + c1, st)
+
+
+def rows(a, r0, r1):
+    return ("ap", a[1], r0, r1, a[4], a[5], a[6])
+
+
+def width(a):
+    return -(-(a[5] - a[4]) // a[6])
+
+
+def build():
+    ops, size, tiles, psn = [], {"F": 0, "H": 0, "J": 0, "U": 0}, {}, [0]
+    cur = [None, -1]
+
+    def tile(pool, key, w):
+        k = (pool, key)
+        if k not in tiles:
+            tiles[k] = ap(pool, size[pool], size[pool] + w)
+            size[pool] += -(-w // 16) * 16
+        return tiles[k]
+
+    def ps():
+        psn[0] += 1
+        return ap(("ps", psn[0]), 0, 512)
+
+    def add(e, ins, rd, wr, **kw):
+        o = dict(e=e, ins=ins, x=cur[0], t=cur[1], rd=[r for r in rd if isinstance(r, tuple)], wr=wr, i=len(ops))
+        o.update(kw)
+        ops.append(o)
+
+    def two(x):
+        return list(x[1:]) if x[0] == "I" else [x]
+
+    def tt(out, a, b, op):
+        add("V", [("tt", out, a, b, op)], two(a) + [b], two(out))
+
+    def ts(out, a, s1, s2, op0, op1=None):
+        add("V", [("ts", out, a, s1, s2, op0, op1)], two(a) + [s1, s2], two(out))
+
+    def cp(out, a):
+        add("V", [("cp", out, a)], two(a) + ([out[2]] if out[0] == "I" else []), [out[1]] if out[0] == "I" else [out])
+
+    def ms(out, v):
+        add("V", [("ms", out, v)], [], [out])
+
+    def scan(out, d0, d1, init, op0, op1):
+        add("V", [("scan", out, d0, d1, init, op0, op1)], [d0, d1], [out])
+
+    def act(out, a, func, bias=0.0, scale=1.0):
+        add("S", [("act", out, a, func, bias, scale)], two(a) + [bias, scale], [out])
+
+    def mm(group):
+        k = len(group)
+        add("P", [("mm", o, l, r, j == 0, j == k - 1) for j, (o, l, r) in enumerate(group)],
+            [x for _, l, r in group for x in (l, r)], [group[0][0]])
+
+    def iota(out, pattern, base, cm):
+        add("G", [("iota", out, pattern, base, cm)], [], [out])
+
+    def asel(out, a, pattern, cmp, fill, base, cm):
+        add("G", [("asel", out, a, pattern, cmp, fill, base, cm)], [a], [out])
+
+    def dma(out, a, eng="Y"):
+        add(eng, [("dma", out, a)], [a], [out], dma=1)
+
+    def send(out, a, key):
+        add("G", [("rd", out, a, key)], [a], [out], dma=1, remote=1)
+
+    D = lambda nm, c1, r1=128: ap(nm, 0, c1, 1, 0, r1)
+    px, vw, vtab, T613, code = ap("pxs", 0, 4096), ap("vws", 0, 2048), ap("vtab", 0, 4096 + n), ap("t613", 0, 4096), ap("code", 0, 4096)
+    v0i, d0i, f0i = tile("J", "v0i", 192), tile("J", "d0i", 192), tile("J", "f0i", 192)
+    wi, ki, z0s = tile("J", "wi", 1), tile("J", "ki", 1), tile("H", "z0s", 192)
+    ms(v0i, 0)
+    ms(d0i, 0)
+    dma(("ap", "J", 0, 128, v0i[4], v0i[5], 1, 16), D("v0", 192, 8))
+    dma(z0s, D("z0", 192), "S")
+    dma(px, D("px", 4096))
+    dma(("ap", "J", 0, 128, d0i[4], d0i[5], 1, 16), D("d0", 192, 8), "S")
+    dma(wi, D("wt", 1), "S")
+    dma(ki, D("kap", 1), "S")
+    dma(f0i, D("f0", 192), "S")
+    dma(vw, D("vw", 2048))
+    ones, B, I = tile("H", "ones", 512), tile("H", "B", 128), tile("H", "I", 128)
+    ms(ones, 1.0)
+    pi = tile("J", "pi", 1)
+    iota(pi, [[0, 1]], 0, 1)
+    kkf = tile("F", "kkf", n)
+    iota(kkf, [[0, 6], [1, 16]], 0, 0)
+    t = tile("H", "Bt", 128)
+    asel(t, sub(ones, 0, 128), [[-16, 8], [0, 16]], "is_ge", 0.0, 0, 1)
+    asel(B, t, [[16, 8], [0, 16]], "is_ge", 0.0, 15, -1)
+    asel(I, sub(ones, 0, 128), [[-1, 128]], "is_equal", 0.0, 0, 1)
+    r6 = tile("F", "r6", 6)
+    iota(r6, [[16, 6]], 0, 0)
+    EXP = tile("H", "EXP", 512)
+    for c in range(3):
+        asel(rows(EXP, 32 * c, 32 * c + 32), rows(ones, 32 * c, 32 * c + 32), [[-1, 32], [0, 16]], "is_equal", 0.0, 0, 1)
+    iota(T613, [[25856, 512], [19616, 8]], 0, 0)
+    TRI, zz = tile("H", "TRI", 4 * n), tile("H", "zz", 4 * n)
+    ms(zz, 0.0)
+    asel(rows(TRI, 0, n), rows(zz, 0, n), [[0, 4], [1, n]], "is_ge", -64.0, -1, -1)
+    lane_i, lane = tile("J", "lane", 1), tile("F", "lane", 1)
+    ts(lane_i, pi, 15, None, "bitwise_and")
+    cp(lane, lane_i)
+    MASK, RST, RSTM = tile("F", "MASK", n), tile("F", "RST", n), tile("F", "RSTM", n)
+    ts(MASK, kkf, lane, None, "is_equal")
+    ts(RSTM, kkf, 0.0, None, "not_equal")
+    B32 = tile("F", "B32", 128)
+    cp(B32, B)
+    v0f = tile("F", "v0f", 192)
+    cp(v0f, v0i)
+    vL, vLf = {}, {}
+
+    def pack_v(x, t_next, P):
+        a, b = tile("F", ("pv", x, t_next), n), tile("F", ("pw", x, t_next), n)
+        tt(a, MASK, P, "mult")
+        scan(b, RSTM, a, 0.0, "mult", "add")
+        return sub(b, 15, n, 16)
+
+    def list_v(x, t, v):
+        vL[x] = tile("U", ("vL", x, t), M6)
+        cp(vL[x], v)
+
+    for x in range(NB):
+        P = ps()
+        mm([(sub(P, 0, n), B32, sub(v0f, x * n, x * n + n))])
+        list_v(x, 0, pack_v(x, 0, sub(P, 0, n)))
+    def scaled(base, s, key):
+        o = tile("H", key, width(base))
+        ts(o, base, float(s), None, "mult")
+        return o
+    SEL, R, GR = tile("H", "SEL", 2048), tile("H", "R", 2048), tile("H", "GR", 1024)
+    nI, Ih, I8, In8, I32, In16, In64, I16, I8192 = [scaled(I, s, ("Is", s)) for s in (-1, .5, 8, -8, 32, -16, -64, 16, 8192)]
+    B2 = scaled(B, 2, "B2")
+    wf, kf, wB = tile("F", "wf", 1), tile("F", "kf", 1), tile("H", "wB", 128)
+    cp(wf, wi)
+    cp(kf, ki)
+    ts(wB, B, wf, None, "mult")
+    Fin, Z, AD = {}, {}, {}
+    d0f = tile("H", "d0f", 192)
+    cp(d0f, d0i)
+    for x in range(NB):
+        Fin[x] = tile("F", ("f0", x), n)
+        cp(Fin[x], sub(f0i, x * n, x * n + n))
+        Z[x] = sub(z0s, x * n, x * n + n)
+        AD[x] = tile("H", ("ad0", x), 2 * n)
+        ms(sub(AD[x], 0, n), 0.0)
+        P = ps()
+        mm([(sub(P, 0, n), B, sub(d0f, x * n, x * n + n))])
+        act(sub(AD[x], n, 2 * n), sub(P, 0, n), "Copy")
+    c0, c1, FL = tile("F", "c0", 1), tile("F", "c1", 1), tile("F", "FL", 16)
+    ts(c0, lane, 12.0, -1.0, "is_lt", "mult")
+    ts(c1, lane, 12.0, None, "is_equal")
+    tt(sub(code, 0, 1), c0, c1, "add")
+    ts(FL, sub(MASK, 0, 16), -2.0, 1.0, "mult", "add")
+    for j in range(12):
+        ts(sub(code, 1 << j, 2 << j), sub(code, 0, 1 << j), sub(FL, j, j + 1), None, "mult")
+    p16, mo, me = tile("J", "p16", 1), tile("F", "mo", 1), tile("F", "me", 1)
+    ts(p16, pi, 4, 1, "logical_shift_right", "bitwise_and")
+    cp(mo, p16)
+    ts(me, mo, -1.0, 1.0, "mult", "add")
+    m12, m12n = tile("F", "m12", 1), tile("F", "m12n", 1)
+    ts(m12, c1, 64.0, None, "mult")
+    ts(m12n, c1, -64.0, None, "mult")
+    kcol = tile("F", "kcol", 16)
+    for q in range(4):
+        ts(sub(kcol, q, q + 1), lane, -2.0, 2.0 * q + 1, "mult", "add")
+    sc, S16, dmp = tile("F", "sc", 6), tile("H", "S16", 6), tile("F", "dmp", 6)
+    ts(sc, r6, lane, None, "add")
+    ts(S16, sc, 16.0, None, "mult")
+    ts(dmp, sc, 4096.0, None, "add")
+    KK = tile("H", "KK", n)
+    cp(KK, kkf)
+    ts(RST, kkf, 0.0, 1e6, "is_equal", "mult")
+    C80, C1, Cq = tile("H", "C80", n), tile("H", "C1", n), tile("H", "Cq", n)
+    ms(C80, 80.0)
+    ms(C1, 1.0)
+    ms(Cq, -0.25)
+    ts(sub(vtab, 0, 2048), vw, 4095, None, "bitwise_and")
+    ts(sub(vtab, 2048, 4096), vw, 12, None, "logical_shift_right")
+    ms(SEL, 0.0)
+    for b in range(16):
+        cp(sub(SEL, b * 128 + b, b * 128 + 128, 16), sub(B, b, 128, 16))
+    NSEL, SEL16 = scaled(SEL, -1, "NSEL"), scaled(SEL, 16, "SEL16")
+    for b in range(16):
+        ts(sub(R, b * 128, b * 128 + 128), B, sub(MASK, b, b + 1), None, "mult")
+    ms(GR, 0.0)
+    for q in range(8):
+        ms(sub(GR, q * 144, q * 144 + 16), 1.0)
+    mat = lambda A, b: sub(A, b * 128, b * 128 + 128)
+    outz, outf, outv, outc = [tile("F", k, 192) for k in ("oz", "of", "ov", "oc")]
+
+    Csave = {}
+    for t in range(4):
+        L, Cx, NLx, over, y, xb, Elist, e0, h, hm, en, src, W, vfs, nxT, nqT, OH1, OH2 = [{} for _ in range(18)]
+        for x in range(NB):
+            cur[0], cur[1] = x, t
+            sent = ("zad", "zland", "vland", "ff", "fland")
+            k = lambda s: (s, x, t if s in sent else t & 1)
+            z = Z[x]
+            y[x], xb[x] = tile("H", k("y"), n), tile("H", k("x"), n)
+            tt(y[x], ("I", px, vL[x]), z, "subtract")
+            act(xb[x], ("I", px, vL[x]), "Copy")
+            a, b = tile("H", k("c1"), n), tile("H", k("c2"), n)
+            ts(a, y[x], 60.0, None, "is_le")
+            ts(b, y[x], -60.0, None, "is_ge")
+            P = ps()
+            grp = []
+            if t == 1:
+                grp = [(sub(P, 0, n), nI, sub(AD[x], 0, n))]
+            elif t > 1:
+                for q in (1.0, 3.0)[:t - 1]:
+                    par = tile("H", k(("par", q)), n)
+                    ts(par, sub(AD[x], 0, n), q, None, "is_equal")
+                    grp.append((sub(P, 0, n), nI, par))
+            mm(grp + [(sub(P, 0, n), B, a), (sub(P, 0, n), B, b)])
+            L[x] = tile("H", k("L"), n)
+            ts(L[x], sub(P, 0, n), 24.0, None, "is_ge")
+            U = ps()
+            mm([(sub(U, 0, n), wB, z)])
+            ui, uj, uh, us = [tile("J", k(("u", q)), n) for q in range(4)]
+            up = tile("F", k("up"), n)
+            cp(ui, sub(U, 0, n))
+            ts(uj, ui, 4095, None, "bitwise_and")
+            ts(up, uj, kf, -15728640.0, "mult", "add")
+            tt(uh, ("I", T613, vL[x]), up, "add")
+            ts(us, uh, 5, 4095, "arith_shift_right", "bitwise_and")
+            hf, m = tile("F", k("hf"), n), ap("vps", 256 * x, 256 * x + n)
+            tt(hf, Fin[x], us, "subtract")
+            tt(m, hf, L[x], "mult")
+            h[x] = tile("F", k("h"), n)
+            tt(h[x], us, m, "add")
+            Hl = tile("U", k("Hl"), n)
+            cp(Hl, h[x])
+            Elist[x] = tile("U", k("El"), n)
+            cp(Elist[x], ("I", vtab, vL[x]))
+            e0[x] = ap("vps", 256 * x + 128, 256 * x + 128 + n)
+            cp(e0[x], Elist[x])
+            Ly = tile("H", k("Ly"), n)
+            tt(Ly, y[x], L[x], "mult")
+            P = ps()
+            mm([(rows(sub(P, 0, 128), 0, n), z, I), (rows(sub(P, 0, 128), 0, n), Ly, I)])
+            nqT[x] = tile("H", k("nqT"), 128)
+            act(rows(nqT[x], 0, n), rows(sub(P, 0, 128), 0, n), "Copy", 0.0, -1.0)
+            P = ps()
+            mm([(rows(sub(P, 0, 128), 0, n), xb[x], I)])
+            nxT[x] = tile("H", k("nxT"), 128)
+            act(rows(nxT[x], 0, n), rows(sub(P, 0, 128), 0, n), "Copy", 0.0, -1.0)
+            da, de = tile("H", ("da", x), 16 * n), tile("H", ("de", x), 16 * n)
+            for which, lst, nT, dist, eng, abse in (("E", Elist[x], nxT[x], de, "V", ABS_E), ("H", Hl, nqT[x], da, "S", ABS_H)):
+                raw = tile("H", ("raw", which, x), 16 * n)
+                for c in range(3):
+                    r, dd = sub(raw, 512 * c, 512 * c + 512), sub(dist, 512 * c, 512 * c + 512)
+                    win = ("I", px, sub(lst, 32 * c, 32 * c + 32))
+                    if eng == "V":
+                        cp(r, win)
+                    else:
+                        act(r, win, "Copy")
+                    P = ps()
+                    mm([(P, I, r), (P, rows(nT, 32 * c, 32 * c + 32), rows(EXP, 32 * c, 32 * c + 32))])
+                    act(dd, P, "Abs")
+            Dp = ps()
+            mm([(sub(Dp, 0, n), I8192, L[x])] + [(sub(Dp, 0, n), mat(SEL, q), sub(de, q, 16 * n, 16)) for q in range(16)])
+            Ds = tile("F", k("Ds"), n)
+            act(Ds, sub(Dp, 0, n), "Copy", -8192.0)
+            kp = ps()
+            mm([(sub(kp, 0, n), I, KK)] + [(sub(kp, 0, n), mat(SEL16, q), sub(da, n * q, n * q + n)) for q in range(16)])
+            Dh = ps()
+            mm([(sub(Dh, 0, n), mat(SEL, q), sub(da, q, 16 * n, 16)) for q in range(16)])
+            P = ps()
+            mm([(sub(P, 0, 2 * n), I, AD[x]), (sub(P, 0, n), I, L[x]), (sub(P, n, 2 * n), In16, L[x]), (sub(P, n, 2 * n), I, C1)])
+            AD1 = tile("H", k("AD1"), 2 * n)
+            act(AD1, sub(P, 0, 2 * n), "Relu")
+            P = ps()
+            mm([(sub(P, 0, n), I, sub(AD1, n, 2 * n)), (sub(P, 0, n, 2), I8, sub(L[x], 1, n, 2)), (sub(P, 1, n, 2), I8, sub(L[x], 0, n, 2))])
+            over[x] = tile("H", k("ov"), n)
+            ts(over[x], sub(P, 0, n), 10.0, None, "is_ge")
+            P = ps()
+            mm([(sub(P, 0, 6), I, S16)] + [(sub(P, 0, 6), mat(NSEL if q & 1 else SEL, q), sub(over[x], q, n, 16)) for q in range(16)])
+            src[x] = tile("U", k("src"), 6)
+            ts(src[x], sub(P, 0, 6), 0.0625, None, "mult")
+            P = ps()
+            mm([(sub(P, 0, n), I, Cq), (sub(P, 0, n), I, z), (sub(P, 0, n), Ih, Ly)])
+            z1 = tile("H", k("z1"), n)
+            ts(z1, sub(P, 0, n), BIGM, BIGM, "add", "subtract")
+            zad = tile("H", k("zad"), 3 * n)
+            if t < 3:
+                act(sub(zad, 0, n), ("I", z1, src[x]), "Copy")
+            else:
+                act(sub(outz, x * n, x * n + n), ("I", z1, src[x]), "Copy")
+            act(sub(zad, n, 2 * n), ("I", sub(AD1, 0, n), src[x]), "Copy")
+            act(sub(zad, 2 * n, 3 * n), ("I", sub(AD1, n, 2 * n), src[x]), "Copy")
+            if t < 3:
+                land = tile("H", k("zland"), 3 * n)
+                send(land, zad, ("z", x, t))
+                Z[x], AD[x] = sub(land, 0, n), sub(land, n, 3 * n)
+            else:
+                P = ps()
+                mm([(sub(P, 0, n), I16, sub(zad, n, 2 * n)), (sub(P, 0, n), I, sub(zad, 2 * n, 3 * n))])
+                act(sub(outc, x * n, x * n + n), sub(P, 0, n), "Copy")
+            P = ps()
+            mm([(sub(P, 0, n), B2, z1), (sub(P, 0, n), nI, L[x])])
+            wi_, w31 = tile("J", k("wi"), n), tile("J", k("w31"), n)
+            ts(wi_, sub(P, 0, n), sub(kcol, t, t + 1), None, "add")
+            ts(w31, wi_, 31, None, "bitwise_and")
+            OH1[x], OH2[x] = tile("F", k("oh1"), n), tile("F", k("oh2"), n)
+            ts(OH1[x], w31, 0.0, None, "is_equal")
+            P = ps()
+            mm([(sub(P, 0, n), I, C80), (sub(P, 0, n, 2), In64, sub(over[x], 1, n, 2)), (sub(P, 1, n, 2), In64, sub(over[x], 0, n, 2))])
+            tt(OH2[x], w31, sub(P, 0, n), "is_equal")
+            hmx = tile("F", k("hm"), n)
+            tt(hmx, h[x], e0[x], "subtract")
+            cc, chm = ap("vps", 256 * x, 256 * x + n), tile("F", k("chm"), n)
+            tt(cc, sub(Dh, 0, n), Ds, "is_lt")
+            tt(chm, hmx, cc, "mult")
+            en[x] = tile("F", k("en"), n)
+            tt(en[x], chm, e0[x], "add")
+            W1, W2, W3 = [tile("F", k(("W", q)), n) for q in range(3)]
+            ks, ki_, kb = tile("J", k("ks"), n), tile("J", k("ki"), 6), tile("H", k("kb"), 6)
+            scan(ks, RST, sub(kp, 0, n), 1e6, "add", "min")
+            ts(ki_, sub(ks, 15, n, 16), 15, None, "bitwise_and")
+            cp(kb, ki_)
+            P = ps()
+            mm([(sub(P, 0, n), I32, L[x]), (sub(P, 0, n), I32, over[x])] + [(sub(P, 6 * q, 6 * q + 6), mat(R, q), kb) for q in range(16)])
+            oh3 = ap("vps", 256 * x, 256 * x + n)
+            ts(oh3, sub(P, 0, n), lane, None, "is_equal")
+            tt(W3, h[x], oh3, "mult")
+            tt(W1, OH1[x], en[x], "mult")
+            tt(sub(W2, 0, n, 2), sub(OH2[x], 1, n, 2), sub(en[x], 1, n, 2), "mult")
+            tt(sub(W2, 1, n, 2), sub(OH2[x], 0, n, 2), sub(en[x], 0, n, 2), "mult")
+            P = ps()
+            mm([(sub(P, 0, n), B32, w) for w in (W1, W2, W3)])
+            vold = vL[x]
+            if t < 3:
+                ff, land = sub(tile("F", k("ff"), n + 16), 0, n + M6), sub(tile("F", k("fland"), n + 16), 0, n + M6)
+                act(sub(ff, 0, n), ("I", en[x], src[x]), "Copy")
+                cp(sub(ff, n, n + M6), pack_v(x, t + 1, sub(P, 0, n)))
+                send(land, ff, ("f", x, t))
+                Fin[x] = sub(land, 0, n)
+                list_v(x, t + 1, sub(land, n, n + M6))
+            else:
+                act(sub(outv, x * n, x * n + n), sub(P, 0, n), "Copy")
+                act(sub(outf, x * n, x * n + n), ("I", en[x], src[x]), "Copy")
+            C, Ce, Co, nl = [tile("H", k(("C", q)), n) for q in range(4)]
+            act(C, ("I", code, vold), "Copy")
+            ts(Ce, C, me, None, "mult")
+            ts(Co, C, mo, None, "mult")
+            ts(nl, L[x], m12, m12n, "mult", "add")
+            Cn = tile("H", k("Cn"), n)
+            tt(Cn, C, nl, "add")
+            Csave[x] = (Cn,)
+            cnt = []
+            for x2 in range(x + 1):
+                E = tile("H", k(("E", x2)), 8 * n)
+                for pb in range(4):
+                    P = ps()
+                    o = rows(sub(P, 0, 2 * n), 0, n)
+                    same = x2 == x
+                    grp = [("mm", o, rows(sub(I, 0, n), 0, n), rows(sub(TRI, 0, 2 * n), 0, n), True, False)] if same else []
+                    for q in range(2):
+                        oo = rows(sub(P, n * q, n * q + n), 0, n)
+                        r = rows(Co if q else Ce, 32 * pb, 32 * pb + 32)
+                        for w, l in enumerate(Csave[x2]):
+                            grp.append(("mm", oo, rows(l, 32 * pb, 32 * pb + 32), r, not same, not same or q == 1))
+                    add("P", grp, [I, TRI, Ce, Co] + list(Csave[x2]), [o])
+                    act(rows(sub(E, 2 * n * pb, 2 * n * pb + 2 * n), 0, n), o, "Relu", -12.0)
+                cnt += [(rows(mat(GR, q), 0, n), rows(sub(E, n * q, n * q + n), 0, n)) for q in range(8)]
+            P = ps()
+            mm([(sub(P, 0, n), In8, L[x])] + [(sub(P, 0, n), l, r) for l, r in cnt])
+            win = tile("H", k("win"), n)
+            ts(win, sub(P, 0, n), -7.5, None, "is_lt")
+            P = ps()
+            mm([(sub(P, 0, 6), mat(SEL, q), sub(win, q, n, 16)) for q in range(16)])
+            vf, vmd, tq, off = [tile("F", k(("o", q)), 6) for q in range(4)]
+            ts(vf, vold, 0.0625, None, "mult")
+            ts(vmd, dmp, -0.0625, None, "mult")
+            tt(vmd, vmd, vf, "add")
+            tt(tq, vmd, sub(P, 0, 6), "mult")
+            tt(off, tq, dmp, "add")
+            W[x] = tile("U", k("off"), 6)
+            cp(W[x], off)
+        for x in range(NB):
+            cp(("I", vtab, W[x]), en[x])
+    cur[0], cur[1] = None, 4
+    for o, nm in ((outz, "yz"), (outf, "yf")):
+        dma(D(nm, 192), o)
+    for o, nm in ((outv, "yv"), (outc, "yc")):
+        dma(D(nm, 192, 8), ("ap", "F", 0, 128, o[4], o[5], 1, 16))
+    for c in range(4):
+        q = ap("vps", 0, 512)
+        o = tile("F", ("yw", c), 512)
+        ts(q, sub(vtab, 2048 + 512 * c, 2560 + 512 * c), 4096.0, None, "mult")
+        tt(o, sub(vtab, 512 * c, 512 * c + 512), q, "add")
+        dma(ap("yw", 512 * c, 512 * c + 512), o, "YS"[c & 1])
+    return ops, size
+
+
+def pat(a):
+    return a[7] if len(a) > 7 else 1
+
+
+def cost(o):
+    c = 0.0
+    for i in o["ins"]:
+        k = i[0]
+        if k == "mm":
+            f = 4 if i[2][1] == "F" else 1
+            c += f * max(64, width(i[3])) * .42e-3
+        elif k in ("iota", "asel"):
+            c += .15 + 1.7e-3 * width(i[1])
+        elif k == "dma":
+            c += .06
+        elif k == "rd":
+            c += .8
+        else:
+            out = i[1][1] if i[1][0] == "I" else i[1]
+            w = width(i[2][2]) * 16 if k != "ms" and i[2][0] == "I" else width(out)
+            b16 = lambda a: a[0] != "I" and a[1] in ("H", "U", "code")
+            if i[1][0] == "I":
+                w = 3.5 * width(i[1][2]) * 16
+            elif k != "ms" and i[2][0] == "I":
+                w = 1.5 * w
+            elif k == "tt":
+                ps_ = any(isinstance(a[1], tuple) or a[1] == "vps" for a in i[2:4])
+                w = w * (1 if ps_ else 2)
+            elif k in ("cp", "ts") and b16(i[1]) and b16(i[2]) or k == "ms" and b16(i[1]):
+                w = w * .5
+            c += max(64, w) * .83e-3 + (.01 if i[2:] else 0)
+    return c
+
+
+WAKE, OWN, NET, LOADT = .12, .06, 2.6, 2.0
+BIAS = 3.0
+
+
+def plan():
+    ops, size = build()
+    N = len(ops)
+    hist = {}
+    deps = [set() for _ in range(N)]
+    tile_ops = {}
+    for o in ops:
+        i = o["i"] = ops.index(o) if ops[o["i"]] is not o else o["i"]
+    for o in ops:
+        i = o["i"]
+        for kind, lst in (("r", o["rd"]), ("w", o["wr"])):
+            for a in lst:
+                buf = a[1]
+                if isinstance(buf, tuple):
+                    tile_ops.setdefault(buf, [])
+                    if i not in tile_ops[buf]:
+                        tile_ops[buf].append(i)
+                for (lo, hi, k2, j, st) in hist.setdefault(buf, []):
+                    if j != i and (k2 == "w" or kind == "w") and lo < a[5] and a[4] < hi:
+                        if st == a[6] > 1 and (lo - a[4]) % st:
+                            continue
+                        deps[i].add(j)
+        for kind, lst in (("r", o["rd"]), ("w", o["wr"])):
+            for a in lst:
+                hh = hist[a[1]]
+                if kind == "w":
+                    hist[a[1]] = hh = [e for e in hh if not (a[6] == 1 and a[2] == 0 and a[3] == 128 and pat(a) == 1 and a[4] <= e[0] and e[1] <= a[5] and a[1] != "vtab")]
+                hh.append((a[4], a[5], kind, i, a[6]))
+    pool = [o["i"] for o in ops if o["e"] == "G" and not o.get("dma")]
+    for a, b in zip(pool, pool[1:]):
+        deps[b].add(a)
+    cst = [cost(o) for o in ops]
+    lat = []
+    for o in ops:
+        if o.get("remote"):
+            lat.append(NET)
+        elif o.get("dma"):
+            w = max(width(a) for a in o["wr"])
+            lat.append(LOADT + w * 1.1e-3)
+        else:
+            lat.append(0.0)
+    prio = [0.0] * N
+    succ = [[] for _ in range(N)]
+    for i in range(N):
+        for j in deps[i]:
+            succ[j].append(i)
+    for i in range(N - 1, -1, -1):
+        prio[i] = cst[i] + lat[i] + max([prio[s] + .1 for s in succ[i]] + [0.0])
+    for i in range(N):
+        prio[i] += BIAS * (ops[i]["x"] == 0)
+    bank_tiles = [[] for _ in range(7)]
+    bank_of, left = {}, {b: len(v) for b, v in tile_ops.items()}
+    fin, free = [None] * N, {}
+    start = [None] * N
+    order = {e: [] for e in "VSPGY"}
+    ndep = [len(d) for d in deps]
+    ready = [i for i in range(N) if ndep[i] == 0]
+    rt = {i: 0.0 for i in ready}
+    extra = [set() for _ in range(N)]
+    done = 0
+    while done < N:
+        best = None
+        for i in ready:
+            o = ops[i]
+            s = max(free.get(o["e"], 0.0), rt[i])
+            bk = None
+            pt = [a[1] for a in o["wr"] if isinstance(a[1], tuple)]
+            if pt and pt[0] not in bank_of:
+                cand = []
+                for b in range(7):
+                    bt = bank_tiles[b]
+                    if not bt or left[bt[-1]] == 0:
+                        f = max([fin[j] for j in tile_ops[bt[-1]]]) + WAKE if bt else 0.0
+                        cand.append((f, b))
+                if not cand:
+                    continue
+                f, bk = min(cand)
+                s = max(s, f)
+            key = (round(s / .04), -prio[i], i)
+            if best is None or key < best[0]:
+                best = (key, s, i, bk)
+        key, s, i, bk = best
+        o = ops[i]
+        ready.remove(i)
+        if bk is not None:
+            tb = [a[1] for a in o["wr"] if isinstance(a[1], tuple)][0]
+            if bank_tiles[bk]:
+                extra[i] |= set(tile_ops[bank_tiles[bk][-1]])
+            bank_tiles[bk].append(tb)
+            bank_of[tb] = bk
+        for tb in set(a[1] for a in o["rd"] + o["wr"] if isinstance(a[1], tuple)):
+            left[tb] -= 1
+        start[i], fin[i] = s, s + cst[i] + lat[i]
+        free[o["e"]] = s + cst[i]
+        order[o["e"]].append(i)
+        done += 1
+        for q in succ[i]:
+            w = OWN if ops[q]["e"] == o["e"] and not o.get("dma") else WAKE
+            rt[q] = max(rt.get(q, 0.0), fin[i] + w)
+            ndep[q] -= 1
+            if ndep[q] == 0:
+                ready.append(q)
+    seq = sorted(range(N), key=lambda i: (start[i], i))
+    cnt = {e: 0 for e in "VSPG"}
+    end, K, clk, waits = {}, {e: {} for e in "VSPGY"}, [None] * N, [None] * N
+    ndma = 0
+    for e in "VSPGY":
+        pos = {i: p for p, i in enumerate(order[e])}
+        for i in order[e]:
+            if ops[i].get("dma"):
+                end[i] = (("d", ndma), 0)
+                ndma += 1
+            else:
+                cnt[e] += len(ops[i]["ins"])
+                end[i] = (e, cnt[e])
+    todo = {e: list(order[e]) for e in order}
+    emitted = set()
+    while any(todo.values()):
+        moved = False
+        for e in "VSPGY":
+            while todo[e] and all(d in emitted for d in deps[todo[e][0]] | extra[todo[e][0]]):
+                i = todo[e].pop(0)
+                ws = []
+                dd = sorted(deps[i] | extra[i], key=lambda d: -fin[d])
+                for d in dd:
+                    s, c = end[d]
+                    if K[e].get(s, -1) >= c:
+                        continue
+                    ws.append(d)
+                    for a, b in clk[d].items():
+                        K[e][a] = max(K[e].get(a, -1), b)
+                fw = {}
+                for d in ws:
+                    s, c = end[d]
+                    if s not in fw or end[fw[s]][1] < c:
+                        fw[s] = d
+                waits[i] = list(fw.values())
+                c = dict(K[e])
+                c[end[i][0]] = max(c.get(end[i][0], -1), end[i][1])
+                clk[i] = c
+                emitted.add(i)
+                moved = True
+        assert moved
+    return dict(ops=ops, size=size, order=order, waits=waits, end=end, bank_of=bank_of, cnt=cnt, ndma=ndma, span=max(fin), start=start, fin=fin, cst=cst)
+
+
+PLAN = plan()
+_s = PLAN["size"]
+SCRATCH = {
+    "pxs": ("sbuf", [128, 4096], "bfloat16"), "vws": ("sbuf", [128, 2048], "int32"), "vtab": ("sbuf", [128, 4096 + n], "int32"),
+    "t613": ("sbuf", [128, 4096], "float32"), "code": ("sbuf", [128, 4096], "bfloat16"),
+}
+for _k in "FHJU":
+    SCRATCH[_k + "pool"] = ("sbuf", [128, _s[_k]], DT[_k])
+for _k in range(7):
+    SCRATCH["ps%d" % _k] = ("psum", [128, 512], "float32")
+SCRATCH["vps"] = ("psum", [128, 512], "float32")
+SEMAPHORES = ["eV", "eS", "eP", "eG", "sent"] + ["d%d" % k for k in range(PLAN["ndma"])]
+
+
+def rank_program(g, core, T, topo):
+    rank = T.rank_of(core)
+    if rank is None:
+        return
+    p = PLAN
+    ops, bank_of, end = p["ops"], p["bank_of"], p["end"]
+    q = {"V": g.vector, "S": g.scalar, "P": g.tensor, "G": g, "Y": g.sync}
+    esem = {e: T.sem["e" + e] for e in "VSPG"}
+    dst = T.cores[(rank + 3) % 8]
+    rid, pid, _ = topo.addr(dst)
+    mask, neng = topo.mask(core, dst), len(topo.engines(core, dst))
+
+    def A(a):
+        if not isinstance(a, tuple):
+            return a
+        if a[0] == "I":
+            return A(a[1]).indirect(A(a[2]))
+        buf = a[1]
+        if isinstance(buf, tuple):
+            t = T["ps%d" % bank_of[buf]]
+        elif buf in DT:
+            t = T[buf + "pool"]
+        else:
+            t = T[buf]
+        if pat(a) > 1:
+            return t[a[2]:a[3]:a[7], a[4]:a[5]]
+        return t[a[2]:a[3], a[4]:a[5]] if a[6] == 1 else t[a[2]:a[3], a[4]:a[5]:a[6]]
+
+    def op(s):
+        return {"add": OP.add, "subtract": OP.subtract, "mult": OP.mult, "min": OP.min, "max": OP.max, "is_ge": OP.is_ge, "is_le": OP.is_le,
+                "is_lt": OP.is_lt, "is_equal": OP.is_equal, "not_equal": OP.not_equal, "bitwise_and": OP.bitwise_and,
+                "arith_shift_right": OP.arith_shift_right, "logical_shift_right": OP.logical_shift_right}[s]
+
+    fun = {"Copy": AF.Copy, "Abs": AF.Abs, "Relu": AF.Relu, "Identity": AF.Identity}
+    nsent = 0
+    total = {}
+    for e in "VSPGY":
+        for i in p["order"][e]:
+            o = ops[i]
+            for d in p["waits"][i]:
+                s, c = end[d]
+                if s in esem:
+                    q[e].wait_ge(esem[s], c)
+                else:
+                    q[e].wait_ge(T.sem["d%d" % s[1]], neng if ops[d].get("remote") else 16)
+            for s in o["ins"]:
+                k = s[0]
+                if k == "dma":
+                    x = q[e].dma_start(A(s[1]), A(s[2]))
+                    x.then_inc(T.sem["d%d" % end[i][0][1]], 16)
+                    total[end[i][0][1]] = 16
+                    continue
+                if k == "rd":
+                    g.remote_dma(out_ap=A(s[1]), in_ap=A(s[2]), remote_sem=T.sem["d%d" % end[i][0][1]], local_sem=T.sem.sent, pid=pid, routing_id=rid, dma_engine_mask=mask)
+                    nsent += neng
+                    total[end[i][0][1]] = neng
+                    continue
+                if k == "tt":
+                    x = g.vector.tensor_tensor(out=A(s[1]), in0=A(s[2]), in1=A(s[3]), op=op(s[4]))
+                elif k == "ts":
+                    if s[6] is None:
+                        x = g.vector.tensor_scalar(out=A(s[1]), in0=A(s[2]), scalar1=A(s[3]), scalar2=None, op0=op(s[5]))
+                    else:
+                        x = g.vector.tensor_scalar(out=A(s[1]), in0=A(s[2]), scalar1=A(s[3]), scalar2=A(s[4]), op0=op(s[5]), op1=op(s[6]))
+                elif k == "cp":
+                    x = g.vector.tensor_copy(out=A(s[1]), in_=A(s[2]))
+                elif k == "ms":
+                    x = g.vector.memset(A(s[1]), s[2])
+                elif k == "scan":
+                    x = g.vector.tensor_tensor_scan(out=A(s[1]), data0=A(s[2]), data1=A(s[3]), initial=s[4], op0=op(s[5]), op1=op(s[6]))
+                elif k == "act":
+                    x = g.scalar.activation(out=A(s[1]), in_=A(s[2]), func=fun[s[3]], bias=A(s[4]), scale=A(s[5]))
+                elif k == "mm":
+                    x = g.tensor.matmul(out=A(s[1]), lhsT=A(s[2]), rhs=A(s[3]), start=s[4], stop=s[5])
+                elif k == "iota":
+                    if s[1][1] in ("F", "H", "t613"):
+                        x = g.iota(out=A(s[1]), pattern=s[2], base=s[3], channel_multiplier=s[4], allow_small_or_imprecise_dtypes=True)
+                    else:
+                        x = g.iota(out=A(s[1]), pattern=s[2], base=s[3], channel_multiplier=s[4])
+                elif k == "asel":
+                    x = g.affine_select(out=A(s[1]), in_=A(s[2]), pattern=s[3], compare_op=op(s[4]), fill=s[5], base=s[6], channel_multiplier=s[7])
+                x.then_inc(esem[e], 1)
+    for e in "VSPG":
+        g.wait_ge(esem[e], p["cnt"][e])
+    for k in sorted(total):
+        g.wait_ge(T.sem["d%d" % k], total[k])
+    g.wait_ge(T.sem.sent, nsent)

@@ -1,5 +1,7 @@
 from concourse.mybir import AluOpType as OP, ActivationFunctionType as AF
 
+import numpy as np
+
 NB, n = 2, 96
 M6, BIGM = 6, 12582912.0
 DT = {"F": "float32", "H": "bfloat16", "J": "int32", "U": "uint16"}
@@ -25,7 +27,7 @@ def width(a):
 
 def build():
     ops, size, tiles, psn = [], {"F": 0, "H": 0, "J": 0, "U": 0}, {}, [0]
-    cur = [None, -1]
+    cur = [None, -1, "setup"]
 
     def tile(pool, key, w):
         k = (pool, key)
@@ -39,7 +41,7 @@ def build():
         return ap(("ps", psn[0]), 0, 512)
 
     def add(e, ins, rd, wr, **kw):
-        o = dict(e=e, ins=ins, x=cur[0], t=cur[1], rd=[r for r in rd if isinstance(r, tuple)], wr=wr, i=len(ops))
+        o = dict(e=e, ins=ins, x=cur[0], t=cur[1], sec=cur[2], rd=[r for r in rd if isinstance(r, tuple)], wr=wr, i=len(ops))
         o.update(kw)
         ops.append(o)
 
@@ -60,6 +62,9 @@ def build():
 
     def scan(out, d0, d1, init, op0, op1):
         add("V", [("scan", out, d0, d1, init, op0, op1)], [d0, d1], [out])
+
+    def tr(out, a):
+        add("V", [("tr", out, a)], [a], [out])
 
     def act(out, a, func, bias=0.0, scale=1.0):
         add("S", [("act", out, a, func, bias, scale)], two(a) + [bias, scale], [out])
@@ -101,6 +106,7 @@ def build():
     iota(pi, [[0, 1]], 0, 1)
     kkf = tile("F", "kkf", n)
     iota(kkf, [[0, 6], [1, 16]], 0, 0)
+    iota(sub(T613, 0, 64), [[25856, 8], [19616, 8]], 0, 0)
     t = tile("H", "Bt", 128)
     asel(t, sub(ones, 0, 128), [[-16, 8], [0, 16]], "is_ge", 0.0, 0, 1)
     asel(B, t, [[16, 8], [0, 16]], "is_ge", 0.0, 15, -1)
@@ -110,10 +116,8 @@ def build():
     EXP = tile("H", "EXP", 512)
     for c in range(3):
         asel(rows(EXP, 32 * c, 32 * c + 32), rows(ones, 32 * c, 32 * c + 32), [[-1, 32], [0, 16]], "is_equal", 0.0, 0, 1)
-    iota(T613, [[25856, 512], [19616, 8]], 0, 0)
-    TRI, zz = tile("H", "TRI", 4 * n), tile("H", "zz", 4 * n)
-    ms(zz, 0.0)
-    asel(rows(TRI, 0, n), rows(zz, 0, n), [[0, 4], [1, n]], "is_ge", -64.0, -1, -1)
+    for j in range(6, 12):
+        act(sub(T613, 1 << j, 2 << j), sub(T613, 0, 1 << j), "Copy", float(3232 << j))
     lane_i, lane = tile("J", "lane", 1), tile("F", "lane", 1)
     ts(lane_i, pi, 15, None, "bitwise_and")
     cp(lane, lane_i)
@@ -133,7 +137,7 @@ def build():
         return sub(b, 15, n, 16)
 
     def list_v(x, t, v):
-        vL[x] = tile("U", ("vL", x, t), M6)
+        vL[x], vLf[x] = tile("U", ("vL", x, t), M6), v
         cp(vL[x], v)
 
     for x in range(NB):
@@ -144,8 +148,8 @@ def build():
         o = tile("H", key, width(base))
         ts(o, base, float(s), None, "mult")
         return o
-    SEL, R, GR = tile("H", "SEL", 2048), tile("H", "R", 2048), tile("H", "GR", 1024)
-    nI, Ih, I8, In8, I32, In16, In64, I16, I8192 = [scaled(I, s, ("Is", s)) for s in (-1, .5, 8, -8, 32, -16, -64, 16, 8192)]
+    SEL, LAST, GR = tile("H", "SEL", 2048), tile("F", "LAST", 128), tile("H", "GR", 1024)
+    nI, Ih, I8, In8, IBIG, In16, In64, I16, I8192 = [scaled(I, s, ("Is", s)) for s in (-1, .5, 8, -8, 131072, -16, -64, 16, 8192)]
     B2 = scaled(B, 2, "B2")
     wf, kf, wB = tile("F", "wf", 1), tile("F", "kf", 1), tile("H", "wB", 128)
     cp(wf, wi)
@@ -169,7 +173,10 @@ def build():
     tt(sub(code, 0, 1), c0, c1, "add")
     ts(FL, sub(MASK, 0, 16), -2.0, 1.0, "mult", "add")
     for j in range(12):
-        ts(sub(code, 1 << j, 2 << j), sub(code, 0, 1 << j), sub(FL, j, j + 1), None, "mult")
+        if j < 10:
+            ts(sub(code, 1 << j, 2 << j), sub(code, 0, 1 << j), sub(FL, j, j + 1), None, "mult")
+        else:
+            act(sub(code, 1 << j, 2 << j), sub(code, 0, 1 << j), "Copy", 0.0, sub(FL, j, j + 1))
     p16, mo, me = tile("J", "p16", 1), tile("F", "mo", 1), tile("F", "me", 1)
     ts(p16, pi, 4, 1, "logical_shift_right", "bitwise_and")
     cp(mo, p16)
@@ -184,8 +191,6 @@ def build():
     ts(sc, r6, lane, None, "add")
     ts(S16, sc, 16.0, None, "mult")
     ts(dmp, sc, 4096.0, None, "add")
-    KK = tile("H", "KK", n)
-    cp(KK, kkf)
     ts(RST, kkf, 0.0, 1e6, "is_equal", "mult")
     C80, C1, Cq = tile("H", "C80", n), tile("H", "C1", n), tile("H", "Cq", n)
     ms(C80, 80.0)
@@ -196,9 +201,9 @@ def build():
     ms(SEL, 0.0)
     for b in range(16):
         cp(sub(SEL, b * 128 + b, b * 128 + 128, 16), sub(B, b, 128, 16))
-    NSEL, SEL16 = scaled(SEL, -1, "NSEL"), scaled(SEL, 16, "SEL16")
-    for b in range(16):
-        ts(sub(R, b * 128, b * 128 + 128), B, sub(MASK, b, b + 1), None, "mult")
+    NSEL = tile("H", "NSEL", 2048)
+    act(NSEL, SEL, "Copy", 0.0, -1.0)
+    ts(LAST, B32, sub(MASK, 15, 16), None, "mult")
     ms(GR, 0.0)
     for q in range(8):
         ms(sub(GR, q * 144, q * 144 + 16), 1.0)
@@ -209,13 +214,13 @@ def build():
     for t in range(4):
         L, Cx, NLx, over, y, xb, Elist, e0, h, hm, en, src, W, vfs, nxT, nqT, OH1, OH2 = [{} for _ in range(18)]
         for x in range(NB):
-            cur[0], cur[1] = x, t
+            cur[:] = [x, t, "like"]
             sent = ("zad", "zland", "vland", "ff", "fland")
             k = lambda s: (s, x, t if s in sent else t & 1)
             z = Z[x]
-            y[x], xb[x] = tile("H", k("y"), n), tile("H", k("x"), n)
-            tt(y[x], ("I", px, vL[x]), z, "subtract")
+            y[x], xb[x] = sub(ps(), 0, n), tile("H", k("x"), n)
             act(xb[x], ("I", px, vL[x]), "Copy")
+            mm([(y[x], nI, z), (y[x], I, xb[x])])
             a, b = tile("H", k("c1"), n), tile("H", k("c2"), n)
             ts(a, y[x], 60.0, None, "is_le")
             ts(b, y[x], -60.0, None, "is_ge")
@@ -231,6 +236,7 @@ def build():
             mm(grp + [(sub(P, 0, n), B, a), (sub(P, 0, n), B, b)])
             L[x] = tile("H", k("L"), n)
             ts(L[x], sub(P, 0, n), 24.0, None, "is_ge")
+            cur[2] = "hash"
             U = ps()
             mm([(sub(U, 0, n), wB, z)])
             ui, uj, uh, us = [tile("J", k(("u", q)), n) for q in range(4)]
@@ -240,17 +246,20 @@ def build():
             ts(up, uj, kf, -15728640.0, "mult", "add")
             tt(uh, ("I", T613, vL[x]), up, "add")
             ts(us, uh, 5, 4095, "arith_shift_right", "bitwise_and")
-            hf, m = tile("F", k("hf"), n), ap("vps", 256 * x, 256 * x + n)
+            vp = "vps%d" % x
+            hf, m = ap(vp, 384, 384 + n), ap(vp, 0, n)
             tt(hf, Fin[x], us, "subtract")
             tt(m, hf, L[x], "mult")
             h[x] = tile("F", k("h"), n)
             tt(h[x], us, m, "add")
             Hl = tile("U", k("Hl"), n)
             cp(Hl, h[x])
+            cur[2] = "E"
             Elist[x] = tile("U", k("El"), n)
             cp(Elist[x], ("I", vtab, vL[x]))
-            e0[x] = ap("vps", 256 * x + 128, 256 * x + 128 + n)
+            e0[x] = ap(vp, 96, 96 + n)
             cp(e0[x], Elist[x])
+            cur[2] = "q"
             Ly = tile("H", k("Ly"), n)
             tt(Ly, y[x], L[x], "mult")
             P = ps()
@@ -263,6 +272,7 @@ def build():
             act(rows(nxT[x], 0, n), rows(sub(P, 0, 128), 0, n), "Copy", 0.0, -1.0)
             da, de = tile("H", ("da", x), 16 * n), tile("H", ("de", x), 16 * n)
             for which, lst, nT, dist, eng, abse in (("E", Elist[x], nxT[x], de, "V", ABS_E), ("H", Hl, nqT[x], da, "S", ABS_H)):
+                cur[2] = which
                 raw = tile("H", ("raw", which, x), 16 * n)
                 for c in range(3):
                     r, dd = sub(raw, 512 * c, 512 * c + 512), sub(dist, 512 * c, 512 * c + 512)
@@ -278,10 +288,9 @@ def build():
             mm([(sub(Dp, 0, n), I8192, L[x])] + [(sub(Dp, 0, n), mat(SEL, q), sub(de, q, 16 * n, 16)) for q in range(16)])
             Ds = tile("F", k("Ds"), n)
             act(Ds, sub(Dp, 0, n), "Copy", -8192.0)
-            kp = ps()
-            mm([(sub(kp, 0, n), I, KK)] + [(sub(kp, 0, n), mat(SEL16, q), sub(da, n * q, n * q + n)) for q in range(16)])
             Dh = ps()
             mm([(sub(Dh, 0, n), mat(SEL, q), sub(da, q, 16 * n, 16)) for q in range(16)])
+            cur[2] = "count"
             P = ps()
             mm([(sub(P, 0, 2 * n), I, AD[x]), (sub(P, 0, n), I, L[x]), (sub(P, n, 2 * n), In16, L[x]), (sub(P, n, 2 * n), I, C1)])
             AD1 = tile("H", k("AD1"), 2 * n)
@@ -313,39 +322,43 @@ def build():
                 P = ps()
                 mm([(sub(P, 0, n), I16, sub(zad, n, 2 * n)), (sub(P, 0, n), I, sub(zad, 2 * n, 3 * n))])
                 act(sub(outc, x * n, x * n + n), sub(P, 0, n), "Copy")
+            cur[2] = "place"
             P = ps()
             mm([(sub(P, 0, n), B2, z1), (sub(P, 0, n), nI, L[x])])
             wi_, w31 = tile("J", k("wi"), n), tile("J", k("w31"), n)
             ts(wi_, sub(P, 0, n), sub(kcol, t, t + 1), None, "add")
             ts(w31, wi_, 31, None, "bitwise_and")
-            OH1[x], OH2[x] = tile("F", k("oh1"), n), tile("F", k("oh2"), n)
+            OH1[x], OH2[x] = ap(vp, 192, 192 + n), ap(vp, 288, 288 + n)
             ts(OH1[x], w31, 0.0, None, "is_equal")
             P = ps()
             mm([(sub(P, 0, n), I, C80), (sub(P, 0, n, 2), In64, sub(over[x], 1, n, 2)), (sub(P, 1, n, 2), In64, sub(over[x], 0, n, 2))])
             tt(OH2[x], w31, sub(P, 0, n), "is_equal")
+            cur[2] = "e"
             hmx = tile("F", k("hm"), n)
             tt(hmx, h[x], e0[x], "subtract")
-            cc, chm = ap("vps", 256 * x, 256 * x + n), tile("F", k("chm"), n)
+            cc, chm = ap(vp, 0, n), tile("F", k("chm"), n)
             tt(cc, sub(Dh, 0, n), Ds, "is_lt")
             tt(chm, hmx, cc, "mult")
             en[x] = tile("F", k("en"), n)
             tt(en[x], chm, e0[x], "add")
             W1, W2, W3 = [tile("F", k(("W", q)), n) for q in range(3)]
-            ks, ki_, kb = tile("J", k("ks"), n), tile("J", k("ki"), 6), tile("H", k("kb"), 6)
-            scan(ks, RST, sub(kp, 0, n), 1e6, "add", "min")
-            ts(ki_, sub(ks, 15, n, 16), 15, None, "bitwise_and")
-            cp(kb, ki_)
+            cur[2] = "least"
+            key, k1, k2, k3 = [tile("F", k(("key", q)), n) for q in range(4)]
+            ts(key, sub(Dh, 0, n), 16.0, lane, "mult", "add")
+            tr(k1, key)
+            scan(k2, RST, k1, 1e6, "add", "min")
+            tr(k3, k2)
             P = ps()
-            mm([(sub(P, 0, n), I32, L[x]), (sub(P, 0, n), I32, over[x])] + [(sub(P, 6 * q, 6 * q + 6), mat(R, q), kb) for q in range(16)])
-            oh3 = ap("vps", 256 * x, 256 * x + n)
-            ts(oh3, sub(P, 0, n), lane, None, "is_equal")
+            mm([(sub(P, 0, n), IBIG, L[x]), (sub(P, 0, n), IBIG, over[x]), (sub(P, 0, n), LAST, k3)])
+            oh3 = ap(vp, 0, n)
+            tt(oh3, key, sub(P, 0, n), "is_equal")
             tt(W3, h[x], oh3, "mult")
             tt(W1, OH1[x], en[x], "mult")
             tt(sub(W2, 0, n, 2), sub(OH2[x], 1, n, 2), sub(en[x], 1, n, 2), "mult")
             tt(sub(W2, 1, n, 2), sub(OH2[x], 0, n, 2), sub(en[x], 0, n, 2), "mult")
             P = ps()
             mm([(sub(P, 0, n), B32, w) for w in (W1, W2, W3)])
-            vold = vL[x]
+            vold, vfold = vL[x], vLf[x]
             if t < 3:
                 ff, land = sub(tile("F", k("ff"), n + 16), 0, n + M6), sub(tile("F", k("fland"), n + 16), 0, n + M6)
                 act(sub(ff, 0, n), ("I", en[x], src[x]), "Copy")
@@ -356,7 +369,9 @@ def build():
             else:
                 act(sub(outv, x * n, x * n + n), sub(P, 0, n), "Copy")
                 act(sub(outf, x * n, x * n + n), ("I", en[x], src[x]), "Copy")
-            C, Ce, Co, nl = [tile("H", k(("C", q)), n) for q in range(4)]
+            cur[2] = "write"
+            C, Ce, Co = [tile("H", k(("C", q)), n) for q in range(3)]
+            nl = ap(vp, 384, 384 + n)
             act(C, ("I", code, vold), "Copy")
             ts(Ce, C, me, None, "mult")
             ts(Co, C, mo, None, "mult")
@@ -371,38 +386,39 @@ def build():
                     P = ps()
                     o = rows(sub(P, 0, 2 * n), 0, n)
                     same = x2 == x
-                    grp = [("mm", o, rows(sub(I, 0, n), 0, n), rows(sub(TRI, 0, 2 * n), 0, n), True, False)] if same else []
+                    grp = []
                     for q in range(2):
                         oo = rows(sub(P, n * q, n * q + n), 0, n)
                         r = rows(Co if q else Ce, 32 * pb, 32 * pb + 32)
                         for w, l in enumerate(Csave[x2]):
-                            grp.append(("mm", oo, rows(l, 32 * pb, 32 * pb + 32), r, not same, not same or q == 1))
-                    add("P", grp, [I, TRI, Ce, Co] + list(Csave[x2]), [o])
+                            grp.append(("mm", oo, rows(l, 32 * pb, 32 * pb + 32), r, True, True))
+                    add("P", grp, [Ce, Co] + list(Csave[x2]), [o])
                     act(rows(sub(E, 2 * n * pb, 2 * n * pb + 2 * n), 0, n), o, "Relu", -12.0)
+                if same:
+                    asel(rows(E, 0, n), rows(E, 0, n), [[0, 8], [1, n]], "is_ge", 0.0, -1, -1)
                 cnt += [(rows(mat(GR, q), 0, n), rows(sub(E, n * q, n * q + n), 0, n)) for q in range(8)]
             P = ps()
             mm([(sub(P, 0, n), In8, L[x])] + [(sub(P, 0, n), l, r) for l, r in cnt])
             win = tile("H", k("win"), n)
-            ts(win, sub(P, 0, n), -7.5, None, "is_lt")
+            ts(win, sub(P, 0, n), -7.5, 0.0625, "is_lt", "mult")
             P = ps()
             mm([(sub(P, 0, 6), mat(SEL, q), sub(win, q, n, 16)) for q in range(16)])
-            vf, vmd, tq, off = [tile("F", k(("o", q)), 6) for q in range(4)]
-            ts(vf, vold, 0.0625, None, "mult")
-            ts(vmd, dmp, -0.0625, None, "mult")
-            tt(vmd, vmd, vf, "add")
+            vmd, tq, off = [tile("F", k(("o", q)), 6) for q in range(3)]
+            tt(vmd, vfold, dmp, "subtract")
             tt(tq, vmd, sub(P, 0, 6), "mult")
             tt(off, tq, dmp, "add")
             W[x] = tile("U", k("off"), 6)
             cp(W[x], off)
         for x in range(NB):
+            cur[:] = [x, t, "write"]
             cp(("I", vtab, W[x]), en[x])
-    cur[0], cur[1] = None, 4
+    cur[:] = [None, 4, "out"]
     for o, nm in ((outz, "yz"), (outf, "yf")):
         dma(D(nm, 192), o)
     for o, nm in ((outv, "yv"), (outc, "yc")):
         dma(D(nm, 192, 8), ("ap", "F", 0, 128, o[4], o[5], 1, 16))
     for c in range(4):
-        q = ap("vps", 0, 512)
+        q = ap("vps%d" % (c & 1), 0, 512)
         o = tile("F", ("yw", c), 512)
         ts(q, sub(vtab, 2048 + 512 * c, 2560 + 512 * c), 4096.0, None, "mult")
         tt(o, sub(vtab, 512 * c, 512 * c + 512), q, "add")
@@ -436,7 +452,7 @@ def cost(o):
             elif k != "ms" and i[2][0] == "I":
                 w = 1.5 * w
             elif k == "tt":
-                ps_ = any(isinstance(a[1], tuple) or a[1] == "vps" for a in i[2:4])
+                ps_ = any(isinstance(a[1], tuple) or a[1] in ("vps0", "vps1") for a in i[2:4])
                 w = w * (1 if ps_ else 2)
             elif k in ("cp", "ts") and b16(i[1]) and b16(i[2]) or k == "ms" and b16(i[1]):
                 w = w * .5
@@ -445,10 +461,15 @@ def cost(o):
 
 
 WAKE, OWN, NET, LOADT = .12, .06, 2.6, 2.0
-BIAS = 3.0
+SCALE = 1.2
+SECT = {("E", 0): 2.6, ("H", 0): 2.9, ("count", 0): 7.3, ("e", 0): 3.0, ("hash", 0): 3.0, ("least", 0): 1.9, ("like", 0): 3.0, ("place", 0): 4.3,
+        ("q", 0): 3.0, ("write", 0): 3.0, ("hash", 1): -0.5, ("E", 1): -2.5, ("H", 1): -2.0, ("out", None): -20.2, ("q", 1): 0.7, ("like", 1): 4.2,
+        ("place", 1): 4.6, ("count", 1): 0.5}
+SEEDS = [(977194, 0.004, 8.0), (73801, 0.004, 8.0), (621379, 0.03, 3.0), (792181, 0.004, 1.0), (493328, 0.004, 3.0), (139368, 0.01, 1.0),
+         (828585, 0.01, 3.0), (445549, 0.03, 1.0), (186910, 0.03, 1.0), (256747, 0.004, 3.0), (625478, 0.01, 1.0), (890177, 0.01, 1.0)]
 
 
-def plan():
+def analyse():
     ops, size = build()
     N = len(ops)
     hist = {}
@@ -479,7 +500,7 @@ def plan():
     pool = [o["i"] for o in ops if o["e"] == "G" and not o.get("dma")]
     for a, b in zip(pool, pool[1:]):
         deps[b].add(a)
-    cst = [cost(o) for o in ops]
+    cst = [cost(o) * (1.0 if o.get("dma") else SCALE) for o in ops]
     lat = []
     for o in ops:
         if o.get("remote"):
@@ -497,8 +518,27 @@ def plan():
     for i in range(N - 1, -1, -1):
         prio[i] = cst[i] + lat[i] + max([prio[s] + .1 for s in succ[i]] + [0.0])
     for i in range(N):
-        prio[i] += BIAS * (ops[i]["x"] == 0)
-    bank_tiles = [[] for _ in range(7)]
+        prio[i] += SECT.get((ops[i]["sec"], ops[i]["x"]), 0.0)
+    return dict(ops=ops, size=size, deps=deps, succ=succ, tile_ops=tile_ops, cst=cst, lat=lat, prio=prio)
+
+
+def nudge(prio, seeds):
+    prio = list(prio)
+    for s, frac, sig in seeds:
+        r = np.random.default_rng(s)
+        hit, by = r.random(len(prio)) < frac, r.normal(size=len(prio)) * sig
+        prio = [float(p + b) if h else p for p, h, b in zip(prio, hit, by)]
+    return prio
+
+
+def schedule(an, prio):
+    ops, deps, succ, tile_ops, cst, lat = an["ops"], an["deps"], an["succ"], an["tile_ops"], an["cst"], an["lat"]
+    N = len(ops)
+    ptile = [next((a[1] for a in o["wr"] if isinstance(a[1], tuple)), None) for o in ops]
+    ptouch = [set(a[1] for a in o["rd"] + o["wr"] if isinstance(a[1], tuple)) for o in ops]
+    eng = [o["e"] for o in ops]
+    isdma = [bool(o.get("dma")) for o in ops]
+    bank_tiles = [[] for _ in range(6)]
     bank_of, left = {}, {b: len(v) for b, v in tile_ops.items()}
     fin, free = [None] * N, {}
     start = [None] * N
@@ -511,13 +551,13 @@ def plan():
     while done < N:
         best = None
         for i in ready:
-            o = ops[i]
-            s = max(free.get(o["e"], 0.0), rt[i])
+            s = max(free.get(eng[i], 0.0), rt[i])
             bk = None
-            pt = [a[1] for a in o["wr"] if isinstance(a[1], tuple)]
-            if pt and pt[0] not in bank_of:
+            if best is not None and round(s / .04) > best[0][0]:
+                continue
+            if ptile[i] is not None and ptile[i] not in bank_of:
                 cand = []
-                for b in range(7):
+                for b in range(6):
                     bt = bank_tiles[b]
                     if not bt or left[bt[-1]] == 0:
                         f = max([fin[j] for j in tile_ops[bt[-1]]]) + WAKE if bt else 0.0
@@ -533,24 +573,31 @@ def plan():
         o = ops[i]
         ready.remove(i)
         if bk is not None:
-            tb = [a[1] for a in o["wr"] if isinstance(a[1], tuple)][0]
+            tb = ptile[i]
             if bank_tiles[bk]:
                 extra[i] |= set(tile_ops[bank_tiles[bk][-1]])
             bank_tiles[bk].append(tb)
             bank_of[tb] = bk
-        for tb in set(a[1] for a in o["rd"] + o["wr"] if isinstance(a[1], tuple)):
+        for tb in ptouch[i]:
             left[tb] -= 1
         start[i], fin[i] = s, s + cst[i] + lat[i]
         free[o["e"]] = s + cst[i]
         order[o["e"]].append(i)
         done += 1
         for q in succ[i]:
-            w = OWN if ops[q]["e"] == o["e"] and not o.get("dma") else WAKE
+            w = OWN if eng[q] == eng[i] and not isdma[i] else WAKE
             rt[q] = max(rt.get(q, 0.0), fin[i] + w)
             ndep[q] -= 1
             if ndep[q] == 0:
                 ready.append(q)
-    seq = sorted(range(N), key=lambda i: (start[i], i))
+    return dict(order=order, start=start, fin=fin, extra=extra, bank_of=bank_of, span=max(fin))
+
+
+def plan():
+    an = analyse()
+    sc = schedule(an, nudge(an["prio"], SEEDS))
+    ops, deps, order, extra, fin = an["ops"], an["deps"], sc["order"], sc["extra"], sc["fin"]
+    N = len(ops)
     cnt = {e: 0 for e in "VSPG"}
     end, K, clk, waits = {}, {e: {} for e in "VSPGY"}, [None] * N, [None] * N
     ndma = 0
@@ -591,7 +638,7 @@ def plan():
                 emitted.add(i)
                 moved = True
         assert moved
-    return dict(ops=ops, size=size, order=order, waits=waits, end=end, bank_of=bank_of, cnt=cnt, ndma=ndma, span=max(fin), start=start, fin=fin, cst=cst)
+    return dict(ops=ops, size=an["size"], order=order, waits=waits, end=end, bank_of=sc["bank_of"], cnt=cnt, ndma=ndma, span=sc["span"])
 
 
 PLAN = plan()
@@ -602,9 +649,8 @@ SCRATCH = {
 }
 for _k in "FHJU":
     SCRATCH[_k + "pool"] = ("sbuf", [128, _s[_k]], DT[_k])
-for _k in range(7):
-    SCRATCH["ps%d" % _k] = ("psum", [128, 512], "float32")
-SCRATCH["vps"] = ("psum", [128, 512], "float32")
+for _k in ["ps%d" % _b for _b in range(6)] + ["vps0", "vps1"]:
+    SCRATCH[_k] = ("psum", [128, 512], "float32")
 SEMAPHORES = ["eV", "eS", "eP", "eG", "sent"] + ["d%d" % k for k in range(PLAN["ndma"])]
 
 
@@ -674,6 +720,8 @@ def rank_program(g, core, T, topo):
                         x = g.vector.tensor_scalar(out=A(s[1]), in0=A(s[2]), scalar1=A(s[3]), scalar2=A(s[4]), op0=op(s[5]), op1=op(s[6]))
                 elif k == "cp":
                     x = g.vector.tensor_copy(out=A(s[1]), in_=A(s[2]))
+                elif k == "tr":
+                    x = g.vector.transpose(out=A(s[1]), in_=A(s[2]))
                 elif k == "ms":
                     x = g.vector.memset(A(s[1]), s[2])
                 elif k == "scan":

from concourse.mybir import AluOpType as OP, ActivationFunctionType as AF

import numpy as np

NB, n = 2, 96
M6, BIGM = 6, 12582912.0
DT = {"F": "float32", "H": "bfloat16", "J": "int32", "U": "uint16"}
EPE = True
ABS_E, ABS_H = "SSS", "SSS"


def ap(buf, c0, c1, st=1, r0=0, r1=128):
    return ("ap", buf, r0, r1, c0, c1, st)


def sub(a, c0, c1, st=1):
    return ("ap", a[1], a[2], a[3], a[4] + c0, a[4] + c1, st)


def rows(a, r0, r1):
    return ("ap", a[1], r0, r1, a[4], a[5], a[6])


def width(a):
    return -(-(a[5] - a[4]) // a[6])


def build():
    ops, size, tiles, psn = [], {"F": 0, "H": 0, "J": 0, "U": 0}, {}, [0]
    cur = [None, -1, "setup"]

    def tile(pool, key, w):
        k = (pool, key)
        if k not in tiles:
            tiles[k] = ap(pool, size[pool], size[pool] + w)
            size[pool] += -(-w // 16) * 16
        return tiles[k]

    def ps():
        psn[0] += 1
        return ap(("ps", psn[0]), 0, 512)

    def add(e, ins, rd, wr, **kw):
        o = dict(e=e, ins=ins, x=cur[0], t=cur[1], sec=cur[2], rd=[r for r in rd if isinstance(r, tuple)], wr=wr, i=len(ops))
        o.update(kw)
        ops.append(o)

    def two(x):
        return list(x[1:]) if x[0] == "I" else [x]

    def tt(out, a, b, op):
        add("V", [("tt", out, a, b, op)], two(a) + [b], two(out))

    def ts(out, a, s1, s2, op0, op1=None):
        add("V", [("ts", out, a, s1, s2, op0, op1)], two(a) + [s1, s2], two(out))

    def cp(out, a):
        add("V", [("cp", out, a)], two(a) + ([out[2]] if out[0] == "I" else []), [out[1]] if out[0] == "I" else [out])

    def ms(out, v):
        add("V", [("ms", out, v)], [], [out])

    def scan(out, d0, d1, init, op0, op1):
        add("V", [("scan", out, d0, d1, init, op0, op1)], [d0, d1], [out])

    def tr(out, a):
        add("V", [("tr", out, a)], [a], [out])

    def act(out, a, func, bias=0.0, scale=1.0):
        add("S", [("act", out, a, func, bias, scale)], two(a) + [bias, scale], [out])

    def mm(group):
        k = len(group)
        add("P", [("mm", o, l, r, j == 0, j == k - 1) for j, (o, l, r) in enumerate(group)],
            [x for _, l, r in group for x in (l, r)], [group[0][0]])

    def iota(out, pattern, base, cm):
        add("G", [("iota", out, pattern, base, cm)], [], [out])

    def asel(out, a, pattern, cmp, fill, base, cm):
        add("G", [("asel", out, a, pattern, cmp, fill, base, cm)], [a], [out])

    def dma(out, a, eng="Y"):
        add(eng, [("dma", out, a)], [a], [out], dma=1)

    def send(out, a, key):
        add("G", [("rd", out, a, key)], [a], [out], dma=1, remote=1)

    D = lambda nm, c1, r1=128: ap(nm, 0, c1, 1, 0, r1)
    px, vw, vtab, T613, code = ap("pxs", 0, 4096), ap("vws", 0, 2048), ap("vtab", 0, 4096 + n), ap("t613", 0, 4096), ap("code", 0, 4096)
    v0i, d0i, f0i = tile("J", "v0i", 192), tile("J", "d0i", 192), tile("J", "f0i", 192)
    wi, ki, z0s = tile("J", "wi", 1), tile("J", "ki", 1), tile("H", "z0s", 192)
    ms(v0i, 0)
    ms(d0i, 0)
    dma(("ap", "J", 0, 128, v0i[4], v0i[5], 1, 16), D("v0", 192, 8))
    dma(z0s, D("z0", 192), "S")
    dma(px, D("px", 4096))
    dma(("ap", "J", 0, 128, d0i[4], d0i[5], 1, 16), D("d0", 192, 8), "S")
    dma(wi, D("wt", 1), "S")
    dma(ki, D("kap", 1), "S")
    dma(f0i, D("f0", 192), "S")
    dma(vw, D("vw", 2048))
    ones, B, I = tile("H", "ones", 512), tile("H", "B", 128), tile("H", "I", 128)
    ms(ones, 1.0)
    pi = tile("J", "pi", 1)
    iota(pi, [[0, 1]], 0, 1)
    kkf = tile("F", "kkf", n)
    iota(kkf, [[0, 6], [1, 16]], 0, 0)
    iota(sub(T613, 0, 64), [[25856, 8], [19616, 8]], 0, 0)
    t = tile("H", "Bt", 128)
    asel(t, sub(ones, 0, 128), [[-16, 8], [0, 16]], "is_ge", 0.0, 0, 1)
    asel(B, t, [[16, 8], [0, 16]], "is_ge", 0.0, 15, -1)
    asel(I, sub(ones, 0, 128), [[-1, 128]], "is_equal", 0.0, 0, 1)
    r6 = tile("F", "r6", 6)
    iota(r6, [[16, 6]], 0, 0)
    EXP = tile("H", "EXP", 512)
    for c in range(3):
        asel(rows(EXP, 32 * c, 32 * c + 32), rows(ones, 32 * c, 32 * c + 32), [[-1, 32], [0, 16]], "is_equal", 0.0, 0, 1)
    for j in range(6, 12):
        act(sub(T613, 1 << j, 2 << j), sub(T613, 0, 1 << j), "Copy", float(3232 << j))
    lane_i, lane = tile("J", "lane", 1), tile("F", "lane", 1)
    ts(lane_i, pi, 15, None, "bitwise_and")
    cp(lane, lane_i)
    MASK, RST, RSTM = tile("F", "MASK", n), tile("F", "RST", n), tile("F", "RSTM", n)
    ts(MASK, kkf, lane, None, "is_equal")
    ts(RSTM, kkf, 0.0, None, "not_equal")
    B32 = tile("F", "B32", 128)
    cp(B32, B)
    v0f = tile("F", "v0f", 192)
    cp(v0f, v0i)
    vL, vLf = {}, {}

    def pack_v(x, t_next, P):
        a, b = tile("F", ("pv", x, t_next), n), tile("F", ("pw", x, t_next), n)
        tt(a, MASK, P, "mult")
        scan(b, RSTM, a, 0.0, "mult", "add")
        return sub(b, 15, n, 16)

    def list_v(x, t, v):
        vL[x], vLf[x] = tile("U", ("vL", x, t), M6), v
        cp(vL[x], v)

    for x in range(NB):
        P = ps()
        mm([(sub(P, 0, n), B32, sub(v0f, x * n, x * n + n))])
        list_v(x, 0, pack_v(x, 0, sub(P, 0, n)))
    def scaled(base, s, key):
        o = tile("H", key, width(base))
        ts(o, base, float(s), None, "mult")
        return o
    SEL, LAST, GR = tile("H", "SEL", 2048), tile("F", "LAST", 128), tile("H", "GR", 1024)
    nI, Ih, I8, In8, IBIG, In16, In64, I16, I8192 = [scaled(I, s, ("Is", s)) for s in (-1, .5, 8, -8, 131072, -16, -64, 16, 8192)]
    B2 = scaled(B, 2, "B2")
    wf, kf, wB = tile("F", "wf", 1), tile("F", "kf", 1), tile("H", "wB", 128)
    cp(wf, wi)
    cp(kf, ki)
    ts(wB, B, wf, None, "mult")
    Fin, Z, AD = {}, {}, {}
    d0f = tile("H", "d0f", 192)
    cp(d0f, d0i)
    for x in range(NB):
        Fin[x] = tile("F", ("f0", x), n)
        cp(Fin[x], sub(f0i, x * n, x * n + n))
        Z[x] = sub(z0s, x * n, x * n + n)
        AD[x] = tile("H", ("ad0", x), 2 * n)
        ms(sub(AD[x], 0, n), 0.0)
        P = ps()
        mm([(sub(P, 0, n), B, sub(d0f, x * n, x * n + n))])
        act(sub(AD[x], n, 2 * n), sub(P, 0, n), "Copy")
    c0, c1, FL = tile("F", "c0", 1), tile("F", "c1", 1), tile("F", "FL", 16)
    ts(c0, lane, 12.0, -1.0, "is_lt", "mult")
    ts(c1, lane, 12.0, None, "is_equal")
    tt(sub(code, 0, 1), c0, c1, "add")
    ts(FL, sub(MASK, 0, 16), -2.0, 1.0, "mult", "add")
    for j in range(12):
        if j < 10:
            ts(sub(code, 1 << j, 2 << j), sub(code, 0, 1 << j), sub(FL, j, j + 1), None, "mult")
        else:
            act(sub(code, 1 << j, 2 << j), sub(code, 0, 1 << j), "Copy", 0.0, sub(FL, j, j + 1))
    p16, mo, me = tile("J", "p16", 1), tile("F", "mo", 1), tile("F", "me", 1)
    ts(p16, pi, 4, 1, "logical_shift_right", "bitwise_and")
    cp(mo, p16)
    ts(me, mo, -1.0, 1.0, "mult", "add")
    m12, m12n = tile("F", "m12", 1), tile("F", "m12n", 1)
    ts(m12, c1, 64.0, None, "mult")
    ts(m12n, c1, -64.0, None, "mult")
    kcol = tile("F", "kcol", 16)
    for q in range(4):
        ts(sub(kcol, q, q + 1), lane, -2.0, 2.0 * q + 1, "mult", "add")
    sc, S16, dmp = tile("F", "sc", 6), tile("H", "S16", 6), tile("F", "dmp", 6)
    ts(sc, r6, lane, None, "add")
    ts(S16, sc, 16.0, None, "mult")
    ts(dmp, sc, 4096.0, None, "add")
    ts(RST, kkf, 0.0, 1e6, "is_equal", "mult")
    C80, C1, Cq = tile("H", "C80", n), tile("H", "C1", n), tile("H", "Cq", n)
    ms(C80, 80.0)
    ms(C1, 1.0)
    ms(Cq, -0.25)
    ts(sub(vtab, 0, 2048), vw, 4095, None, "bitwise_and")
    ts(sub(vtab, 2048, 4096), vw, 12, None, "logical_shift_right")
    ms(SEL, 0.0)
    for b in range(16):
        cp(sub(SEL, b * 128 + b, b * 128 + 128, 16), sub(B, b, 128, 16))
    NSEL = tile("H", "NSEL", 2048)
    act(NSEL, SEL, "Copy", 0.0, -1.0)
    ts(LAST, B32, sub(MASK, 15, 16), None, "mult")
    ms(GR, 0.0)
    for q in range(8):
        ms(sub(GR, q * 144, q * 144 + 16), 1.0)
    mat = lambda A, b: sub(A, b * 128, b * 128 + 128)
    outz, outf, outv, outc = [tile("F", k, 192) for k in ("oz", "of", "ov", "oc")]

    Csave = {}
    for t in range(4):
        L, Cx, NLx, over, y, xb, Elist, e0, h, hm, en, src, W, vfs, nxT, nqT, OH1, OH2 = [{} for _ in range(18)]
        for x in range(NB):
            cur[:] = [x, t, "like"]
            sent = ("zad", "zland", "vland", "ff", "fland")
            k = lambda s: (s, x, t if s in sent else t & 1)
            z = Z[x]
            y[x], xb[x] = sub(ps(), 0, n), tile("H", k("x"), n)
            act(xb[x], ("I", px, vL[x]), "Copy")
            mm([(y[x], nI, z), (y[x], I, xb[x])])
            a, b = tile("H", k("c1"), n), tile("H", k("c2"), n)
            ts(a, y[x], 60.0, None, "is_le")
            ts(b, y[x], -60.0, None, "is_ge")
            P = ps()
            grp = []
            if t == 1:
                grp = [(sub(P, 0, n), nI, sub(AD[x], 0, n))]
            elif t > 1:
                for q in (1.0, 3.0)[:t - 1]:
                    par = tile("H", k(("par", q)), n)
                    ts(par, sub(AD[x], 0, n), q, None, "is_equal")
                    grp.append((sub(P, 0, n), nI, par))
            mm(grp + [(sub(P, 0, n), B, a), (sub(P, 0, n), B, b)])
            L[x] = tile("H", k("L"), n)
            ts(L[x], sub(P, 0, n), 24.0, None, "is_ge")
            cur[2] = "hash"
            U = ps()
            mm([(sub(U, 0, n), wB, z)])
            ui, uj, uh, us = [tile("J", k(("u", q)), n) for q in range(4)]
            up = tile("F", k("up"), n)
            cp(ui, sub(U, 0, n))
            ts(uj, ui, 4095, None, "bitwise_and")
            ts(up, uj, kf, -15728640.0, "mult", "add")
            tt(uh, ("I", T613, vL[x]), up, "add")
            ts(us, uh, 5, 4095, "arith_shift_right", "bitwise_and")
            vp = "vps%d" % x
            hf, m = ap(vp, 384, 384 + n), ap(vp, 0, n)
            tt(hf, Fin[x], us, "subtract")
            tt(m, hf, L[x], "mult")
            h[x] = tile("F", k("h"), n)
            tt(h[x], us, m, "add")
            Hl = tile("U", k("Hl"), n)
            cp(Hl, h[x])
            cur[2] = "E"
            Elist[x] = tile("U", k("El"), n)
            cp(Elist[x], ("I", vtab, vL[x]))
            e0[x] = ap(vp, 96, 96 + n)
            cp(e0[x], Elist[x])
            cur[2] = "q"
            Ly = tile("H", k("Ly"), n)
            tt(Ly, y[x], L[x], "mult")
            P = ps()
            mm([(rows(sub(P, 0, 128), 0, n), z, I), (rows(sub(P, 0, 128), 0, n), Ly, I)])
            nqT[x] = tile("H", k("nqT"), 128)
            act(rows(nqT[x], 0, n), rows(sub(P, 0, 128), 0, n), "Copy", 0.0, -1.0)
            P = ps()
            mm([(rows(sub(P, 0, 128), 0, n), xb[x], I)])
            nxT[x] = tile("H", k("nxT"), 128)
            act(rows(nxT[x], 0, n), rows(sub(P, 0, 128), 0, n), "Copy", 0.0, -1.0)
            da, de = tile("H", ("da", x), 16 * n), tile("H", ("de", x), 16 * n)
            for which, lst, nT, dist, eng, abse in (("E", Elist[x], nxT[x], de, "V", ABS_E), ("H", Hl, nqT[x], da, "S", ABS_H)):
                cur[2] = which
                raw = tile("H", ("raw", which, x), 16 * n)
                for c in range(3):
                    r, dd = sub(raw, 512 * c, 512 * c + 512), sub(dist, 512 * c, 512 * c + 512)
                    win = ("I", px, sub(lst, 32 * c, 32 * c + 32))
                    if eng == "V":
                        cp(r, win)
                    else:
                        act(r, win, "Copy")
                    P = ps()
                    mm([(P, I, r), (P, rows(nT, 32 * c, 32 * c + 32), rows(EXP, 32 * c, 32 * c + 32))])
                    act(dd, P, "Abs")
            Dp = ps()
            mm([(sub(Dp, 0, n), I8192, L[x])] + [(sub(Dp, 0, n), mat(SEL, q), sub(de, q, 16 * n, 16)) for q in range(16)])
            Ds = tile("F", k("Ds"), n)
            act(Ds, sub(Dp, 0, n), "Copy", -8192.0)
            Dh = ps()
            mm([(sub(Dh, 0, n), mat(SEL, q), sub(da, q, 16 * n, 16)) for q in range(16)])
            cur[2] = "count"
            P = ps()
            mm([(sub(P, 0, 2 * n), I, AD[x]), (sub(P, 0, n), I, L[x]), (sub(P, n, 2 * n), In16, L[x]), (sub(P, n, 2 * n), I, C1)])
            AD1 = tile("H", k("AD1"), 2 * n)
            act(AD1, sub(P, 0, 2 * n), "Relu")
            P = ps()
            mm([(sub(P, 0, n), I, sub(AD1, n, 2 * n)), (sub(P, 0, n, 2), I8, sub(L[x], 1, n, 2)), (sub(P, 1, n, 2), I8, sub(L[x], 0, n, 2))])
            over[x] = tile("H", k("ov"), n)
            ts(over[x], sub(P, 0, n), 10.0, None, "is_ge")
            P = ps()
            mm([(sub(P, 0, 6), I, S16)] + [(sub(P, 0, 6), mat(NSEL if q & 1 else SEL, q), sub(over[x], q, n, 16)) for q in range(16)])
            src[x] = tile("U", k("src"), 6)
            ts(src[x], sub(P, 0, 6), 0.0625, None, "mult")
            P = ps()
            mm([(sub(P, 0, n), I, Cq), (sub(P, 0, n), I, z), (sub(P, 0, n), Ih, Ly)])
            z1 = tile("H", k("z1"), n)
            ts(z1, sub(P, 0, n), BIGM, BIGM, "add", "subtract")
            zad = tile("H", k("zad"), 3 * n)
            if t < 3:
                act(sub(zad, 0, n), ("I", z1, src[x]), "Copy")
            else:
                act(sub(outz, x * n, x * n + n), ("I", z1, src[x]), "Copy")
            act(sub(zad, n, 2 * n), ("I", sub(AD1, 0, n), src[x]), "Copy")
            act(sub(zad, 2 * n, 3 * n), ("I", sub(AD1, n, 2 * n), src[x]), "Copy")
            if t < 3:
                land = tile("H", k("zland"), 3 * n)
                send(land, zad, ("z", x, t))
                Z[x], AD[x] = sub(land, 0, n), sub(land, n, 3 * n)
            else:
                P = ps()
                mm([(sub(P, 0, n), I16, sub(zad, n, 2 * n)), (sub(P, 0, n), I, sub(zad, 2 * n, 3 * n))])
                act(sub(outc, x * n, x * n + n), sub(P, 0, n), "Copy")
            cur[2] = "place"
            P = ps()
            mm([(sub(P, 0, n), B2, z1), (sub(P, 0, n), nI, L[x])])
            wi_, w31 = tile("J", k("wi"), n), tile("J", k("w31"), n)
            ts(wi_, sub(P, 0, n), sub(kcol, t, t + 1), None, "add")
            ts(w31, wi_, 31, None, "bitwise_and")
            OH1[x], OH2[x] = ap(vp, 192, 192 + n), ap(vp, 288, 288 + n)
            ts(OH1[x], w31, 0.0, None, "is_equal")
            P = ps()
            mm([(sub(P, 0, n), I, C80), (sub(P, 0, n, 2), In64, sub(over[x], 1, n, 2)), (sub(P, 1, n, 2), In64, sub(over[x], 0, n, 2))])
            tt(OH2[x], w31, sub(P, 0, n), "is_equal")
            cur[2] = "e"
            hmx = tile("F", k("hm"), n)
            tt(hmx, h[x], e0[x], "subtract")
            cc, chm = ap(vp, 0, n), tile("F", k("chm"), n)
            tt(cc, sub(Dh, 0, n), Ds, "is_lt")
            tt(chm, hmx, cc, "mult")
            en[x] = tile("F", k("en"), n)
            tt(en[x], chm, e0[x], "add")
            W1, W2, W3 = [tile("F", k(("W", q)), n) for q in range(3)]
            cur[2] = "least"
            key, k1, k2, k3 = [tile("F", k(("key", q)), n) for q in range(4)]
            ts(key, sub(Dh, 0, n), 16.0, lane, "mult", "add")
            tr(k1, key)
            scan(k2, RST, k1, 1e6, "add", "min")
            tr(k3, k2)
            P = ps()
            mm([(sub(P, 0, n), IBIG, L[x]), (sub(P, 0, n), IBIG, over[x]), (sub(P, 0, n), LAST, k3)])
            oh3 = ap(vp, 0, n)
            tt(oh3, key, sub(P, 0, n), "is_equal")
            tt(W3, h[x], oh3, "mult")
            tt(W1, OH1[x], en[x], "mult")
            tt(sub(W2, 0, n, 2), sub(OH2[x], 1, n, 2), sub(en[x], 1, n, 2), "mult")
            tt(sub(W2, 1, n, 2), sub(OH2[x], 0, n, 2), sub(en[x], 0, n, 2), "mult")
            P = ps()
            mm([(sub(P, 0, n), B32, w) for w in (W1, W2, W3)])
            vold, vfold = vL[x], vLf[x]
            if t < 3:
                ff, land = sub(tile("F", k("ff"), n + 16), 0, n + M6), sub(tile("F", k("fland"), n + 16), 0, n + M6)
                act(sub(ff, 0, n), ("I", en[x], src[x]), "Copy")
                cp(sub(ff, n, n + M6), pack_v(x, t + 1, sub(P, 0, n)))
                send(land, ff, ("f", x, t))
                Fin[x] = sub(land, 0, n)
                list_v(x, t + 1, sub(land, n, n + M6))
            else:
                act(sub(outv, x * n, x * n + n), sub(P, 0, n), "Copy")
                act(sub(outf, x * n, x * n + n), ("I", en[x], src[x]), "Copy")
            cur[2] = "write"
            C, Ce, Co = [tile("H", k(("C", q)), n) for q in range(3)]
            nl = ap(vp, 384, 384 + n)
            act(C, ("I", code, vold), "Copy")
            ts(Ce, C, me, None, "mult")
            ts(Co, C, mo, None, "mult")
            ts(nl, L[x], m12, m12n, "mult", "add")
            Cn = tile("H", k("Cn"), n)
            tt(Cn, C, nl, "add")
            Csave[x] = (Cn,)
            cnt = []
            for x2 in range(x + 1):
                E = tile("H", k(("E", x2)), 8 * n)
                for pb in range(4):
                    P = ps()
                    o = rows(sub(P, 0, 2 * n), 0, n)
                    same = x2 == x
                    grp = []
                    for q in range(2):
                        oo = rows(sub(P, n * q, n * q + n), 0, n)
                        r = rows(Co if q else Ce, 32 * pb, 32 * pb + 32)
                        for w, l in enumerate(Csave[x2]):
                            grp.append(("mm", oo, rows(l, 32 * pb, 32 * pb + 32), r, True, True))
                    add("P", grp, [Ce, Co] + list(Csave[x2]), [o])
                    act(rows(sub(E, 2 * n * pb, 2 * n * pb + 2 * n), 0, n), o, "Relu", -12.0)
                if same:
                    asel(rows(E, 0, n), rows(E, 0, n), [[0, 8], [1, n]], "is_ge", 0.0, -1, -1)
                cnt += [(rows(mat(GR, q), 0, n), rows(sub(E, n * q, n * q + n), 0, n)) for q in range(8)]
            P = ps()
            mm([(sub(P, 0, n), In8, L[x])] + [(sub(P, 0, n), l, r) for l, r in cnt])
            win = tile("H", k("win"), n)
            ts(win, sub(P, 0, n), -7.5, 0.0625, "is_lt", "mult")
            P = ps()
            mm([(sub(P, 0, 6), mat(SEL, q), sub(win, q, n, 16)) for q in range(16)])
            vmd, tq, off = [tile("F", k(("o", q)), 6) for q in range(3)]
            tt(vmd, vfold, dmp, "subtract")
            tt(tq, vmd, sub(P, 0, 6), "mult")
            tt(off, tq, dmp, "add")
            W[x] = tile("U", k("off"), 6)
            cp(W[x], off)
        for x in range(NB):
            cur[:] = [x, t, "write"]
            cp(("I", vtab, W[x]), en[x])
    cur[:] = [None, 4, "out"]
    for o, nm in ((outz, "yz"), (outf, "yf")):
        dma(D(nm, 192), o)
    for o, nm in ((outv, "yv"), (outc, "yc")):
        dma(D(nm, 192, 8), ("ap", "F", 0, 128, o[4], o[5], 1, 16))
    for c in range(4):
        q = ap("vps%d" % (c & 1), 0, 512)
        o = tile("F", ("yw", c), 512)
        ts(q, sub(vtab, 2048 + 512 * c, 2560 + 512 * c), 4096.0, None, "mult")
        tt(o, sub(vtab, 512 * c, 512 * c + 512), q, "add")
        dma(ap("yw", 512 * c, 512 * c + 512), o, "YS"[c & 1])
    return ops, size


def pat(a):
    return a[7] if len(a) > 7 else 1


def cost(o):
    c = 0.0
    for i in o["ins"]:
        k = i[0]
        if k == "mm":
            f = 4 if i[2][1] == "F" else 1
            c += f * max(64, width(i[3])) * .42e-3
        elif k in ("iota", "asel"):
            c += .15 + 1.7e-3 * width(i[1])
        elif k == "dma":
            c += .06
        elif k == "rd":
            c += .8
        else:
            out = i[1][1] if i[1][0] == "I" else i[1]
            w = width(i[2][2]) * 16 if k != "ms" and i[2][0] == "I" else width(out)
            b16 = lambda a: a[0] != "I" and a[1] in ("H", "U", "code")
            if i[1][0] == "I":
                w = 3.5 * width(i[1][2]) * 16
            elif k != "ms" and i[2][0] == "I":
                w = 1.5 * w
            elif k == "tt":
                ps_ = any(isinstance(a[1], tuple) or a[1] in ("vps0", "vps1") for a in i[2:4])
                w = w * (1 if ps_ else 2)
            elif k in ("cp", "ts") and b16(i[1]) and b16(i[2]) or k == "ms" and b16(i[1]):
                w = w * .5
            c += max(64, w) * .83e-3 + (.01 if i[2:] else 0)
    return c


WAKE, OWN, NET, LOADT = .12, .06, 2.6, 2.0
SCALE = 1.2
SECT = {("E", 0): 2.6, ("H", 0): 2.9, ("count", 0): 7.3, ("e", 0): 3.0, ("hash", 0): 3.0, ("least", 0): 1.9, ("like", 0): 3.0, ("place", 0): 4.3,
        ("q", 0): 3.0, ("write", 0): 3.0, ("hash", 1): -0.5, ("E", 1): -2.5, ("H", 1): -2.0, ("out", None): -20.2, ("q", 1): 0.7, ("like", 1): 4.2,
        ("place", 1): 4.6, ("count", 1): 0.5}
SEEDS = [(977194, 0.004, 8.0), (73801, 0.004, 8.0), (621379, 0.03, 3.0), (792181, 0.004, 1.0), (493328, 0.004, 3.0), (139368, 0.01, 1.0),
         (828585, 0.01, 3.0), (445549, 0.03, 1.0), (186910, 0.03, 1.0), (256747, 0.004, 3.0), (625478, 0.01, 1.0), (890177, 0.01, 1.0)]


def analyse():
    ops, size = build()
    N = len(ops)
    hist = {}
    deps = [set() for _ in range(N)]
    tile_ops = {}
    for o in ops:
        i = o["i"] = ops.index(o) if ops[o["i"]] is not o else o["i"]
    for o in ops:
        i = o["i"]
        for kind, lst in (("r", o["rd"]), ("w", o["wr"])):
            for a in lst:
                buf = a[1]
                if isinstance(buf, tuple):
                    tile_ops.setdefault(buf, [])
                    if i not in tile_ops[buf]:
                        tile_ops[buf].append(i)
                for (lo, hi, k2, j, st) in hist.setdefault(buf, []):
                    if j != i and (k2 == "w" or kind == "w") and lo < a[5] and a[4] < hi:
                        if st == a[6] > 1 and (lo - a[4]) % st:
                            continue
                        deps[i].add(j)
        for kind, lst in (("r", o["rd"]), ("w", o["wr"])):
            for a in lst:
                hh = hist[a[1]]
                if kind == "w":
                    hist[a[1]] = hh = [e for e in hh if not (a[6] == 1 and a[2] == 0 and a[3] == 128 and pat(a) == 1 and a[4] <= e[0] and e[1] <= a[5] and a[1] != "vtab")]
                hh.append((a[4], a[5], kind, i, a[6]))
    pool = [o["i"] for o in ops if o["e"] == "G" and not o.get("dma")]
    for a, b in zip(pool, pool[1:]):
        deps[b].add(a)
    cst = [cost(o) * (1.0 if o.get("dma") else SCALE) for o in ops]
    lat = []
    for o in ops:
        if o.get("remote"):
            lat.append(NET)
        elif o.get("dma"):
            w = max(width(a) for a in o["wr"])
            lat.append(LOADT + w * 1.1e-3)
        else:
            lat.append(0.0)
    prio = [0.0] * N
    succ = [[] for _ in range(N)]
    for i in range(N):
        for j in deps[i]:
            succ[j].append(i)
    for i in range(N - 1, -1, -1):
        prio[i] = cst[i] + lat[i] + max([prio[s] + .1 for s in succ[i]] + [0.0])
    for i in range(N):
        prio[i] += SECT.get((ops[i]["sec"], ops[i]["x"]), 0.0)
    return dict(ops=ops, size=size, deps=deps, succ=succ, tile_ops=tile_ops, cst=cst, lat=lat, prio=prio)


def nudge(prio, seeds):
    prio = list(prio)
    for s, frac, sig in seeds:
        r = np.random.default_rng(s)
        hit, by = r.random(len(prio)) < frac, r.normal(size=len(prio)) * sig
        prio = [float(p + b) if h else p for p, h, b in zip(prio, hit, by)]
    return prio


def schedule(an, prio):
    ops, deps, succ, tile_ops, cst, lat = an["ops"], an["deps"], an["succ"], an["tile_ops"], an["cst"], an["lat"]
    N = len(ops)
    ptile = [next((a[1] for a in o["wr"] if isinstance(a[1], tuple)), None) for o in ops]
    ptouch = [set(a[1] for a in o["rd"] + o["wr"] if isinstance(a[1], tuple)) for o in ops]
    eng = [o["e"] for o in ops]
    isdma = [bool(o.get("dma")) for o in ops]
    bank_tiles = [[] for _ in range(6)]
    bank_of, left = {}, {b: len(v) for b, v in tile_ops.items()}
    fin, free = [None] * N, {}
    start = [None] * N
    order = {e: [] for e in "VSPGY"}
    ndep = [len(d) for d in deps]
    ready = [i for i in range(N) if ndep[i] == 0]
    rt = {i: 0.0 for i in ready}
    extra = [set() for _ in range(N)]
    done = 0
    while done < N:
        best = None
        for i in ready:
            s = max(free.get(eng[i], 0.0), rt[i])
            bk = None
            if best is not None and round(s / .04) > best[0][0]:
                continue
            if ptile[i] is not None and ptile[i] not in bank_of:
                cand = []
                for b in range(6):
                    bt = bank_tiles[b]
                    if not bt or left[bt[-1]] == 0:
                        f = max([fin[j] for j in tile_ops[bt[-1]]]) + WAKE if bt else 0.0
                        cand.append((f, b))
                if not cand:
                    continue
                f, bk = min(cand)
                s = max(s, f)
            key = (round(s / .04), -prio[i], i)
            if best is None or key < best[0]:
                best = (key, s, i, bk)
        key, s, i, bk = best
        o = ops[i]
        ready.remove(i)
        if bk is not None:
            tb = ptile[i]
            if bank_tiles[bk]:
                extra[i] |= set(tile_ops[bank_tiles[bk][-1]])
            bank_tiles[bk].append(tb)
            bank_of[tb] = bk
        for tb in ptouch[i]:
            left[tb] -= 1
        start[i], fin[i] = s, s + cst[i] + lat[i]
        free[o["e"]] = s + cst[i]
        order[o["e"]].append(i)
        done += 1
        for q in succ[i]:
            w = OWN if eng[q] == eng[i] and not isdma[i] else WAKE
            rt[q] = max(rt.get(q, 0.0), fin[i] + w)
            ndep[q] -= 1
            if ndep[q] == 0:
                ready.append(q)
    return dict(order=order, start=start, fin=fin, extra=extra, bank_of=bank_of, span=max(fin))


def plan():
    an = analyse()
    sc = schedule(an, nudge(an["prio"], SEEDS))
    ops, deps, order, extra, fin = an["ops"], an["deps"], sc["order"], sc["extra"], sc["fin"]
    N = len(ops)
    cnt = {e: 0 for e in "VSPG"}
    end, K, clk, waits = {}, {e: {} for e in "VSPGY"}, [None] * N, [None] * N
    ndma = 0
    for e in "VSPGY":
        pos = {i: p for p, i in enumerate(order[e])}
        for i in order[e]:
            if ops[i].get("dma"):
                end[i] = (("d", ndma), 0)
                ndma += 1
            else:
                cnt[e] += len(ops[i]["ins"])
                end[i] = (e, cnt[e])
    todo = {e: list(order[e]) for e in order}
    emitted = set()
    while any(todo.values()):
        moved = False
        for e in "VSPGY":
            while todo[e] and all(d in emitted for d in deps[todo[e][0]] | extra[todo[e][0]]):
                i = todo[e].pop(0)
                ws = []
                dd = sorted(deps[i] | extra[i], key=lambda d: -fin[d])
                for d in dd:
                    s, c = end[d]
                    if K[e].get(s, -1) >= c:
                        continue
                    ws.append(d)
                    for a, b in clk[d].items():
                        K[e][a] = max(K[e].get(a, -1), b)
                fw = {}
                for d in ws:
                    s, c = end[d]
                    if s not in fw or end[fw[s]][1] < c:
                        fw[s] = d
                waits[i] = list(fw.values())
                c = dict(K[e])
                c[end[i][0]] = max(c.get(end[i][0], -1), end[i][1])
                clk[i] = c
                emitted.add(i)
                moved = True
        assert moved
    return dict(ops=ops, size=an["size"], order=order, waits=waits, end=end, bank_of=sc["bank_of"], cnt=cnt, ndma=ndma, span=sc["span"])


PLAN = plan()
_s = PLAN["size"]
SCRATCH = {
    "pxs": ("sbuf", [128, 4096], "bfloat16"), "vws": ("sbuf", [128, 2048], "int32"), "vtab": ("sbuf", [128, 4096 + n], "int32"),
    "t613": ("sbuf", [128, 4096], "float32"), "code": ("sbuf", [128, 4096], "bfloat16"),
}
for _k in "FHJU":
    SCRATCH[_k + "pool"] = ("sbuf", [128, _s[_k]], DT[_k])
for _k in ["ps%d" % _b for _b in range(6)] + ["vps0", "vps1"]:
    SCRATCH[_k] = ("psum", [128, 512], "float32")
SEMAPHORES = ["eV", "eS", "eP", "eG", "sent"] + ["d%d" % k for k in range(PLAN["ndma"])]


def rank_program(g, core, T, topo):
    rank = T.rank_of(core)
    if rank is None:
        return
    p = PLAN
    ops, bank_of, end = p["ops"], p["bank_of"], p["end"]
    q = {"V": g.vector, "S": g.scalar, "P": g.tensor, "G": g, "Y": g.sync}
    esem = {e: T.sem["e" + e] for e in "VSPG"}
    dst = T.cores[(rank + 3) % 8]
    rid, pid, _ = topo.addr(dst)
    mask, neng = topo.mask(core, dst), len(topo.engines(core, dst))

    def A(a):
        if not isinstance(a, tuple):
            return a
        if a[0] == "I":
            return A(a[1]).indirect(A(a[2]))
        buf = a[1]
        if isinstance(buf, tuple):
            t = T["ps%d" % bank_of[buf]]
        elif buf in DT:
            t = T[buf + "pool"]
        else:
            t = T[buf]
        if pat(a) > 1:
            return t[a[2]:a[3]:a[7], a[4]:a[5]]
        return t[a[2]:a[3], a[4]:a[5]] if a[6] == 1 else t[a[2]:a[3], a[4]:a[5]:a[6]]

    def op(s):
        return {"add": OP.add, "subtract": OP.subtract, "mult": OP.mult, "min": OP.min, "max": OP.max, "is_ge": OP.is_ge, "is_le": OP.is_le,
                "is_lt": OP.is_lt, "is_equal": OP.is_equal, "not_equal": OP.not_equal, "bitwise_and": OP.bitwise_and,
                "arith_shift_right": OP.arith_shift_right, "logical_shift_right": OP.logical_shift_right}[s]

    fun = {"Copy": AF.Copy, "Abs": AF.Abs, "Relu": AF.Relu, "Identity": AF.Identity}
    nsent = 0
    total = {}
    for e in "VSPGY":
        for i in p["order"][e]:
            o = ops[i]
            for d in p["waits"][i]:
                s, c = end[d]
                if s in esem:
                    q[e].wait_ge(esem[s], c)
                else:
                    q[e].wait_ge(T.sem["d%d" % s[1]], neng if ops[d].get("remote") else 16)
            for s in o["ins"]:
                k = s[0]
                if k == "dma":
                    x = q[e].dma_start(A(s[1]), A(s[2]))
                    x.then_inc(T.sem["d%d" % end[i][0][1]], 16)
                    total[end[i][0][1]] = 16
                    continue
                if k == "rd":
                    g.remote_dma(out_ap=A(s[1]), in_ap=A(s[2]), remote_sem=T.sem["d%d" % end[i][0][1]], local_sem=T.sem.sent, pid=pid, routing_id=rid, dma_engine_mask=mask)
                    nsent += neng
                    total[end[i][0][1]] = neng
                    continue
                if k == "tt":
                    x = g.vector.tensor_tensor(out=A(s[1]), in0=A(s[2]), in1=A(s[3]), op=op(s[4]))
                elif k == "ts":
                    if s[6] is None:
                        x = g.vector.tensor_scalar(out=A(s[1]), in0=A(s[2]), scalar1=A(s[3]), scalar2=None, op0=op(s[5]))
                    else:
                        x = g.vector.tensor_scalar(out=A(s[1]), in0=A(s[2]), scalar1=A(s[3]), scalar2=A(s[4]), op0=op(s[5]), op1=op(s[6]))
                elif k == "cp":
                    x = g.vector.tensor_copy(out=A(s[1]), in_=A(s[2]))
                elif k == "tr":
                    x = g.vector.transpose(out=A(s[1]), in_=A(s[2]))
                elif k == "ms":
                    x = g.vector.memset(A(s[1]), s[2])
                elif k == "scan":
                    x = g.vector.tensor_tensor_scan(out=A(s[1]), data0=A(s[2]), data1=A(s[3]), initial=s[4], op0=op(s[5]), op1=op(s[6]))
                elif k == "act":
                    x = g.scalar.activation(out=A(s[1]), in_=A(s[2]), func=fun[s[3]], bias=A(s[4]), scale=A(s[5]))
                elif k == "mm":
                    x = g.tensor.matmul(out=A(s[1]), lhsT=A(s[2]), rhs=A(s[3]), start=s[4], stop=s[5])
                elif k == "iota":
                    if s[1][1] in ("F", "H", "t613"):
                        x = g.iota(out=A(s[1]), pattern=s[2], base=s[3], channel_multiplier=s[4], allow_small_or_imprecise_dtypes=True)
                    else:
                        x = g.iota(out=A(s[1]), pattern=s[2], base=s[3], channel_multiplier=s[4])
                elif k == "asel":
                    x = g.affine_select(out=A(s[1]), in_=A(s[2]), pattern=s[3], compare_op=op(s[4]), fill=s[5], base=s[6], channel_multiplier=s[7])
                x.then_inc(esem[e], 1)
    for e in "VSPG":
        g.wait_ge(esem[e], p["cnt"][e])
    for k in sorted(total):
        g.wait_ge(T.sem["d%d" % k], total[k])
    g.wait_ge(T.sem.sent, nsent)
